import numpy as np
import ml_dtypes


def mxq(x, axis, fmt="e4m3"):
    dtype, down = {"e4m3": (ml_dtypes.float8_e4m3fn, 7), "e5m2": (ml_dtypes.float8_e5m2, 14)}[fmt]
    v = np.moveaxis(np.asarray(x, np.float32).astype(ml_dtypes.bfloat16).astype(np.float64), axis, -1)
    blocks = v.reshape(v.shape[:-1] + (-1, 32))
    amax = np.abs(blocks).max(-1, keepdims=True)
    byte = np.maximum(np.where(amax > 0, np.frexp(amax)[1] - 1 + 127, 0) - down, 1)
    scale = np.exp2(byte - 127.0)
    codes = (blocks / scale).astype(np.float32).astype(dtype).astype(np.float64)
    return np.moveaxis((codes * scale).reshape(v.shape), -1, axis)


WIDE = False


def mx_kscale(k):
    if not WIDE:
        return np.ones(k)
    levels = np.array([10, -10, 5, -5, 0])
    if k % 512:
        return np.exp2(np.random.permutation(np.resize(levels, k // 32))).repeat(32)
    a = np.empty((k // 512, 16))
    for p in range(k // 512):
        a[p, :8] = np.random.permutation(np.resize(levels, 8))
        for g in range(8):
            far = levels[np.abs(levels - a[p, g]) >= 10]
            a[p, g + 8] = far[np.random.randint(len(far))]
    return np.exp2(a.ravel()).repeat(32)


def f64(x):
    return np.asarray(x).astype(np.float64)


def striped(idx):
    return np.tile(idx.reshape(-1, 16).T, (8, 1)).astype(np.uint16)


def unstriped(offs):
    return offs[:16].T.reshape(-1).astype(np.int64)


E2M1 = np.array([0.0, 0.5, 1.0, 1.5, 2.0, 3.0, 4.0, 6.0, -0.0, -0.5, -1.0, -1.5, -2.0, -3.0, -4.0, -6.0])


def pack_weight(w, fmt):
    k, n = w.shape
    w = f64(np.asarray(w, np.float32).astype(ml_dtypes.bfloat16)).reshape(k // 32, 32, n)
    amax = np.abs(w).max(1)
    if fmt == "e4m3":
        byte = np.frexp(amax)[1] - 1 + 127 - 7
    else:
        mant, ex = np.frexp(amax / 6.0)
        byte = np.where(mant > 0.5, ex, ex - 1) + 127
    byte = np.clip(np.where(amax > 0, byte, 1), 1, 254)
    scaled = (w * np.exp2(127.0 - byte)[:, None, :]).reshape(k, n).astype(np.float32)
    by_word = np.ascontiguousarray(scaled.reshape(k // 512, 128, 4, n).transpose(0, 1, 3, 2))
    if fmt == "e4m3":
        words = by_word.astype(ml_dtypes.float8_e4m3fn).view(np.uint8)
    else:
        c = by_word.astype(ml_dtypes.float4_e2m1fn).view(np.uint8) & 0xF
        words = (c[..., 0::2] | (c[..., 1::2] << 4)).reshape(k // 512, 128, 2 * n)
    return np.ascontiguousarray(words), np.ascontiguousarray(byte.astype(np.uint8).reshape(k // 512, 16, n))


def unpack_weight(words, scales, fmt):
    g, _, n = scales.shape
    words = np.ascontiguousarray(words).reshape(g, 128, n, -1)
    if fmt == "e4m3":
        vals = words.view(ml_dtypes.float8_e4m3fn).astype(np.float64)
    else:
        nib = np.empty((g, 128, n, 4), np.uint8)
        nib[..., 0::2] = words & 0xF
        nib[..., 1::2] = words >> 4
        vals = E2M1[nib]
    vals = vals * np.repeat(np.exp2(scales.astype(np.float64) - 127.0), 8, axis=1)[..., None]
    return vals.transpose(0, 1, 3, 2).reshape(g * 512, n)


def relu(v):
    return np.maximum(v, 0.0)


K, T, E, C, H, N = 512, 1024, 4, 256, 512, 128


def by_expert(wq, xq):
    return np.concatenate([wq[e].T @ xq[:, e * C:(e + 1) * C] for e in range(E)], axis=1)


def setup_inputs():
    n = np.random.standard_normal
    s = mx_kscale(K)
    u = mx_kscale(H)
    slot_token = np.random.permutation(T)[:E * C]
    partner = np.concatenate([np.random.permutation(T) for _ in range(-(-E * C // T))])[:E * C]
    x = pack_weight(n((K, T)) * s[:, None], "e4m3")
    return {
        "x_words": x[0],
        "x_scales": x[1],
        "w1": (n((E, K, H)) / np.sqrt(K) / s[None, :, None] * u).astype(np.float32),
        "wp": (n((E, K, H)) / np.sqrt(K) / s[None, :, None] * u).astype(np.float32),
        "w2": (n((E, H, N)) / np.sqrt(H) / u[None, :, None]).astype(np.float32),
        "gate": np.tile(np.random.uniform(0.2, 1.0, E * C), (128, 1)).astype(np.float32),
        "offs": striped(slot_token),
        "offs2": striped(partner),
    }


def reference(x_words, x_scales, w1, wp, w2, gate, offs, offs2):
    w1q = mxq(f64(w1), 1, "e4m3")
    wpq = mxq(f64(wp), 1, "e4m3")
    w2q = mxq(f64(w2), 1, "e4m3")
    idx, idx2 = unstriped(offs), unstriped(offs2)
    x = unpack_weight(x_words, x_scales, "e4m3")
    h = relu(by_expert(w1q, x[:, idx]) + by_expert(wpq, x[:, idx2]))
    y = by_expert(w2q, mxq(h, 0, "e4m3"))
    out = np.zeros((N, T))
    out[:, idx] = f64(gate[:1]) * y
    return out

@@ -1,0 +1,258 @@
+from contextlib import ExitStack
+
+import concourse.mybir as mybir
+
+K, T, E, C, H, N = 512, 1024, 4, 256, 512, 128
+FLOPS = 2 * E * C * (2 * K * H + H * N)
+
+F32 = mybir.dt.float32
+BF16 = mybir.dt.bfloat16
+I32 = mybir.dt.int32
+U32 = mybir.dt.uint32
+U16 = mybir.dt.uint16
+U8 = mybir.dt.uint8
+FP8X4 = mybir.dt.float8_e4m3fn_x4
+RELU = mybir.ActivationFunctionType.Relu
+MULT = mybir.AluOpType.mult
+
+P = 128
+PACK = 4
+HALF = C // 2
+COLS = H // 2
+PIECE_BYTES = PACK * COLS * 4
+
+
+def tile_moe_duo_relu_kernel(tc, x_words, x_scales, w1, wp, w2, gate, offs, offs2, out):
+    nc = tc.nc
+    with ExitStack() as ctx:
+        keep = ctx.enter_context(tc.tile_pool(name="keep", bufs=1))
+        stage = ctx.enter_context(tc.tile_pool(name="stage", bufs=1))
+        hpsum = ctx.enter_context(tc.psum_pool(name="hpsum", bufs=6))
+        ypsum = ctx.enter_context(tc.psum_pool(name="ypsum", bufs=2))
+
+        lists = [keep.tile([P, T // 16], U16, name="offs_sb"), keep.tile([P, T // 16], U16, name="offs2_sb")]
+        xw = keep.tile([P, T], U32, name="xw", align_bytes=64)
+        xs = keep.tile([P, T], U8, name="xs", align_bytes=64)
+        gate_sb = keep.tile([P, E * C], F32, name="gate_sb", align_bytes=64)
+        out_sb = keep.tile([P, T], F32, name="out_sb", align_bytes=64)
+        raw2 = keep.tile([P, E, PACK, N], F32, name="raw2", align_bytes=64)
+
+        def on_piece(m, h, skip=0):
+            return (2 * m + h) * PIECE_BYTES + skip
+
+        raw = {}
+
+        def load_first(m, h):
+            rows = (w1, wp)[m % 2][m // 2].rearrange("(p j) c -> p j c", j=PACK)
+            raw[m, h] = stage.tile([P, PACK, COLS], F32, name="raw%d%d" % (m, h), align_bytes=64, offset=on_piece(m, h))
+            nc.sync.dma_start(raw[m, h][:], rows[:, :, h * COLS : (h + 1) * COLS])
+
+        def load_second(a, b):
+            nc.sync.dma_start(raw2[:, a:b], w2[a:b].rearrange("e (p j) n -> p e j n", j=PACK))
+
+        def load_gate(a, b):
+            nc.sync.dma_start(gate_sb[:, a * C : b * C], gate[:, a * C : b * C])
+
+        nc.vector.memset(xs[:].bitcast(I32), 0)
+        nc.sync.dma_start(lists[0][:], offs)
+        nc.sync.dma_start(xw[:].bitcast(I32), x_words[0].rearrange("p t d -> p (t d)").bitcast(I32))
+        nc.sync.dma_start(lists[1][:], offs2)
+        for q in range(4):
+            nc.scalar.dma_start(xs[32 * q : 32 * q + 4, :].bitcast(I32), x_scales[0, 4 * q : 4 * q + 4, :].bitcast(I32))
+        load_first(0, 0)
+        load_first(0, 1)
+        load_first(1, 0)
+        load_first(1, 1)
+        load_first(2, 0)
+        load_first(2, 1)
+        load_first(3, 0)
+        load_second(0, 1)
+        load_first(3, 1)
+        load_first(4, 0)
+        load_first(4, 1)
+        load_first(5, 0)
+        load_first(5, 1)
+        load_gate(0, 1)
+        load_first(6, 0)
+        load_first(6, 1)
+        load_second(1, 3)
+        load_first(7, 0)
+        load_first(7, 1)
+        load_second(3, 4)
+        load_gate(1, 4)
+
+        words, scales = {}, {}
+
+        def gather(pair):
+            cols = slice(pair * 2 * C // 16, (pair + 1) * 2 * C // 16)
+            for s in range(2):
+                words[pair, s] = keep.tile([P, 2 * C], U32, name="gw%d%d" % (pair, s), align_bytes=64)
+                nc.vector.tensor_copy(words[pair, s][:], xw[:].indirect(lists[s][:, cols]))
+            for s in range(2):
+                scales[pair, s] = keep.tile([P, 2 * C], U8, name="gs%d%d" % (pair, s), align_bytes=64)
+                nc.vector.tensor_copy(scales[pair, s][:], xs[:].indirect(lists[s][:, cols]))
+
+        grouped = [keep.tile([P, PACK, P, PACK], BF16, name="grp%d" % m, align_bytes=64) for m in range(2 * E)]
+        wc = [keep.tile([P, H], U32, name="wc%d" % m, align_bytes=64) for m in range(2 * E)]
+        ws = [keep.tile([P, H], U8, name="ws%d" % m, align_bytes=64) for m in range(2 * E)]
+
+        def cast(engine, dst, src):
+            if engine == "V":
+                nc.vector.tensor_copy(dst, src)
+            else:
+                nc.scalar.copy(dst, src)
+
+        def cast_first(m, h, engine):
+            dst = grouped[m][:, :, h * 64 : (h + 1) * 64, :].rearrange("p t m j -> p m j t")
+            cast(engine, dst, raw[m, h][:].rearrange("p j (m t) -> p m j t", t=PACK))
+
+        def quantize(codes, plane, values):
+            nc.vector.quantize_mx(out=codes.bitcast(FP8X4), scales=plane, in_=values)
+
+        def quant_first(m, t=None):
+            if t is None:
+                quantize(wc[m][:], ws[m][:], grouped[m][:].rearrange("p t m j -> p (t m j)"))
+            else:
+                quantize(wc[m][:, t * P : (t + 1) * P], ws[m][:, t * P : (t + 1) * P], grouped[m][:, t].rearrange("p m j -> p (m j)"))
+
+        grouped2 = [keep.tile([P, N, PACK], BF16, name="grp2_%d" % e, align_bytes=64)[:] for e in range(E - 1)]
+        grouped2.append(grouped[2 * E - 1][:, PACK - 1])
+        w2c = [keep.tile([P, N], U32, name="w2c%d" % e, align_bytes=64) for e in range(E)]
+        w2s = [keep.tile([P, N], U8, name="w2s%d" % e, align_bytes=64) for e in range(E)]
+
+        def cast_second(e, engine):
+            cast(engine, grouped2[e].rearrange("p (c i) j -> p c j i", i=4), raw2[:, e].rearrange("p j (c i) -> p c j i", i=4))
+
+        def quant_second(e):
+            quantize(w2c[e][:], w2s[e][:], grouped2[e].rearrange("p n j -> p (n j)"))
+
+        hb_at = {0: on_piece(4, 0), 1: on_piece(6, 0), 2: on_piece(7, 0)}
+        ysb_at = {0: on_piece(6, 0, 2048), 1: on_piece(7, 0, 2048)}
+        hb, ysb, acc, yacc = {}, {}, {}, {}
+        hc = [keep.tile([P, C], U32, name="hc%d" % e, align_bytes=64) for e in range(E)]
+        hs = [keep.tile([P, C], U8, name="hs%d" % e, align_bytes=64) for e in range(E)]
+
+        def first_layer(e, u):
+            acc[e, u] = hpsum.tile([P, PACK, HALF], F32, name="acc")
+            slots = slice((e % 2) * C + u * HALF, (e % 2) * C + (u + 1) * HALF)
+            for t in range(PACK):
+                for s in range(2):
+                    nc.tensor.matmul_mx(
+                        out=acc[e, u][:, t, :],
+                        lhsT=wc[2 * e + s][:, t * P : (t + 1) * P].bitcast(FP8X4),
+                        lhsT_scale=ws[2 * e + s][:, t * P : (t + 1) * P],
+                        rhs=words[e // 2, s][:, slots].bitcast(FP8X4),
+                        rhs_scale=scales[e // 2, s][:, slots],
+                        start=(s == 0),
+                        stop=(s == 1),
+                    )
+
+        def relu(e, u):
+            if u == 0:
+                if e in hb_at:
+                    hb[e] = stage.tile([P, C, PACK], BF16, name="hb%d" % e, align_bytes=64, offset=hb_at[e])
+                else:
+                    hb[e] = keep.tile([P, C, PACK], BF16, name="hb%d" % e, align_bytes=64)
+            nc.scalar.activation(hb[e][:, u * HALF : (u + 1) * HALF, :], acc[e, u][:].rearrange("p t n -> p n t"), RELU)
+
+        def quant_hidden(e, a=0, b=C):
+            quantize(hc[e][:, a:b], hs[e][:, a:b], hb[e][:, a:b, :].rearrange("p n t -> p (n t)"))
+
+        def second_layer(e, a=0, b=C):
+            yacc[e, a] = ypsum.tile([P, b - a], F32, name="yacc")
+            nc.tensor.matmul_mx(
+                out=yacc[e, a][:],
+                lhsT=w2c[e][:].bitcast(FP8X4),
+                lhsT_scale=w2s[e][:],
+                rhs=hc[e][:, a:b].bitcast(FP8X4),
+                rhs_scale=hs[e][:, a:b],
+                start=True,
+                stop=True,
+            )
+
+        def copy_out(e, a=0, b=C):
+            if a == 0:
+                if e in ysb_at:
+                    ysb[e] = stage.tile([P, C], F32, name="ysb%d" % e, align_bytes=64, offset=ysb_at[e])
+                else:
+                    ysb[e] = keep.tile([P, C], F32, name="ysb%d" % e, align_bytes=64)
+            nc.scalar.copy(ysb[e][:, a:b], yacc[e, a][:])
+
+        def scatter(e, a=0, b=C):
+            window = out_sb[:].indirect(lists[0][:, (e * C + a) // 16 : (e * C + b) // 16])
+            nc.vector.tensor_tensor(window, ysb[e][:, a:b], gate_sb[:, e * C + a : e * C + b], MULT)
+
+        gather(0)
+        gather(1)
+        cast_first(0, 0, "S")
+        cast_first(0, 1, "S")
+        cast_first(1, 0, "S")
+        cast_first(1, 1, "S")
+        cast_first(2, 0, "S")
+        cast_first(2, 1, "S")
+        cast_first(3, 0, "S")
+        quant_first(0)
+        quant_first(1)
+        cast_second(0, "S")
+        quant_first(2)
+        first_layer(0, 0)
+        cast_first(4, 0, "S")
+        cast_first(3, 1, "V")
+        first_layer(0, 1)
+        quant_first(3)
+        relu(0, 0)
+        quant_second(0)
+        cast_first(4, 1, "V")
+        first_layer(1, 0)
+        relu(0, 1)
+        cast_first(5, 0, "S")
+        quant_first(4)
+        first_layer(1, 1)
+        cast_first(5, 1, "V")
+        quant_hidden(0)
+        cast_first(6, 0, "S")
+        quant_first(5)
+        second_layer(0)
+        first_layer(2, 0)
+        cast_first(6, 1, "V")
+        copy_out(0)
+        relu(1, 0)
+        scatter(0)
+        first_layer(2, 1)
+        relu(1, 1)
+        cast_second(1, "S")
+        cast_second(2, "S")
+        quant_first(6)
+        cast_first(7, 0, "S")
+        quant_hidden(1)
+        quant_second(1)
+        quant_second(2)
+        cast_first(7, 1, "V")
+        second_layer(1)
+        relu(2, 0)
+        quant_first(7, 0)
+        quant_first(7, 1)
+        relu(2, 1)
+        quant_first(7, 2)
+        quant_first(7, 3)
+        first_layer(3, 0)
+        cast_second(3, "V")
+        copy_out(1)
+        quant_hidden(2)
+        quant_second(3)
+        first_layer(3, 1)
+        scatter(1)
+        relu(3, 0)
+        second_layer(2)
+        relu(3, 1)
+        quant_hidden(3, 0, HALF)
+        copy_out(2)
+        quant_hidden(3, HALF, C)
+        second_layer(3, 0, HALF)
+        scatter(2)
+        second_layer(3, HALF, C)
+        copy_out(3, 0, HALF)
+        copy_out(3, HALF, C)
+        scatter(3, 0, HALF)
+        scatter(3, HALF, C)
+        nc.sync.dma_start(out, out_sb[:])

@@ -19,7 +19,7 @@ P = 128
 PACK = 4
 HALF = C // 2
 COLS = H // 2
-PIECE_BYTES = PACK * COLS * 4
+SLOT_BYTES = PACK * COLS * 4
 
 
 def tile_moe_duo_relu_kernel(tc, x_words, x_scales, w1, wp, w2, gate, offs, offs2, out):
@@ -35,133 +35,136 @@ def tile_moe_duo_relu_kernel(tc, x_words, x_scales, w1, wp, w2, gate, offs, offs
         xs = keep.tile([P, T], U8, name="xs", align_bytes=64)
         gate_sb = keep.tile([P, E * C], F32, name="gate_sb", align_bytes=64)
         out_sb = keep.tile([P, T], F32, name="out_sb", align_bytes=64)
-        raw2 = keep.tile([P, E, PACK, N], F32, name="raw2", align_bytes=64)
 
-        def on_piece(m, h, skip=0):
-            return (2 * m + h) * PIECE_BYTES + skip
+        def on_raw(m, h, skip=0):
+            return (2 * m + h) * SLOT_BYTES + skip
 
-        raw = {}
+        def on_rounded(m, skip=0):
+            return (4 * E + m) * SLOT_BYTES + skip
+
+        def on_raw2(e):
+            return (6 * E + e) * SLOT_BYTES
+
+        def placed(shape, dtype, name, at):
+            if at is None:
+                return keep.tile(shape, dtype, name=name, align_bytes=64)
+            return stage.tile(shape, dtype, name=name, align_bytes=64, offset=at)
+
+        raw, raw2 = {}, {}
 
         def load_first(m, h):
             rows = (w1, wp)[m % 2][m // 2].rearrange("(p j) c -> p j c", j=PACK)
-            raw[m, h] = stage.tile([P, PACK, COLS], F32, name="raw%d%d" % (m, h), align_bytes=64, offset=on_piece(m, h))
+            raw[m, h] = placed([P, PACK, COLS], F32, "raw%d%d" % (m, h), on_raw(m, h))
             nc.sync.dma_start(raw[m, h][:], rows[:, :, h * COLS : (h + 1) * COLS])
 
-        def load_second(a, b):
-            nc.sync.dma_start(raw2[:, a:b], w2[a:b].rearrange("e (p j) n -> p e j n", j=PACK))
+        def load_second(e):
+            raw2[e] = placed([P, PACK, N], F32, "raw2_%d" % e, on_raw2(e))
+            nc.sync.dma_start(raw2[e][:], w2[e].rearrange("(p j) n -> p j n", j=PACK))
 
-        def load_gate(a, b):
-            nc.sync.dma_start(gate_sb[:, a * C : b * C], gate[:, a * C : b * C])
+        def load_gate(e):
+            nc.sync.dma_start(gate_sb[:, e * C : (e + 1) * C], gate[:, e * C : (e + 1) * C])
 
-        nc.vector.memset(xs[:].bitcast(I32), 0)
         nc.sync.dma_start(lists[0][:], offs)
-        nc.sync.dma_start(xw[:].bitcast(I32), x_words[0].rearrange("p t d -> p (t d)").bitcast(I32))
-        nc.sync.dma_start(lists[1][:], offs2)
         for q in range(4):
-            nc.scalar.dma_start(xs[32 * q : 32 * q + 4, :].bitcast(I32), x_scales[0, 4 * q : 4 * q + 4, :].bitcast(I32))
-        load_first(0, 0)
-        load_first(0, 1)
-        load_first(1, 0)
-        load_first(1, 1)
-        load_first(2, 0)
-        load_first(2, 1)
-        load_first(3, 0)
-        load_second(0, 1)
-        load_first(3, 1)
-        load_first(4, 0)
-        load_first(4, 1)
-        load_first(5, 0)
-        load_first(5, 1)
-        load_gate(0, 1)
-        load_first(6, 0)
-        load_first(6, 1)
-        load_second(1, 3)
-        load_first(7, 0)
-        load_first(7, 1)
-        load_second(3, 4)
-        load_gate(1, 4)
+            rows = x_scales[0, 4 * q : 4 * q + 4, :].bitcast(I32)
+            nc.sync.dma_start(xs[32 * q : 32 * q + 32, :].bitcast(I32), rows.partition_broadcast(8))
+        nc.sync.dma_start(lists[1][:], offs2)
+        for e in range(E):
+            load_first(2 * e, 0)
+            if e >= 2:
+                load_second(e - 1)
+            load_first(2 * e, 1)
+            if e == 1:
+                load_second(e - 1)
+            load_first(2 * e + 1, 0)
+            if e == 0:
+                nc.sync.dma_start(xw[:].bitcast(I32), x_words[0].rearrange("p t d -> p (t d)").bitcast(I32))
+            load_first(2 * e + 1, 1)
+            if 1 <= e < E - 1:
+                load_gate(e - 1)
+        load_second(E - 1)
+        load_gate(E - 2)
+        load_gate(E - 1)
 
         words, scales = {}, {}
 
-        def gather(pair):
+        def gather(table, dtype, into, label, pair, at=(None, None)):
             cols = slice(pair * 2 * C // 16, (pair + 1) * 2 * C // 16)
             for s in range(2):
-                words[pair, s] = keep.tile([P, 2 * C], U32, name="gw%d%d" % (pair, s), align_bytes=64)
-                nc.vector.tensor_copy(words[pair, s][:], xw[:].indirect(lists[s][:, cols]))
-            for s in range(2):
-                scales[pair, s] = keep.tile([P, 2 * C], U8, name="gs%d%d" % (pair, s), align_bytes=64)
-                nc.vector.tensor_copy(scales[pair, s][:], xs[:].indirect(lists[s][:, cols]))
+                into[pair, s] = placed([P, 2 * C], dtype, "%s%d%d" % (label, pair, s), at[s])
+                nc.vector.tensor_copy(into[pair, s][:], table[:].indirect(lists[s][:, cols]))
 
-        grouped = [keep.tile([P, PACK, P, PACK], BF16, name="grp%d" % m, align_bytes=64) for m in range(2 * E)]
+        grouped = [placed([P, PACK, P, PACK], BF16, "grp%d" % m, on_rounded(m)) for m in range(2 * E)]
         wc = [keep.tile([P, H], U32, name="wc%d" % m, align_bytes=64) for m in range(2 * E)]
         ws = [keep.tile([P, H], U8, name="ws%d" % m, align_bytes=64) for m in range(2 * E)]
 
         def cast(engine, dst, src):
-            if engine == "V":
+            if engine == "G":
+                nc.gpsimd.tensor_copy(dst, src)
+            elif engine == "V":
                 nc.vector.tensor_copy(dst, src)
             else:
                 nc.scalar.copy(dst, src)
 
         def cast_first(m, h, engine):
+            src = raw[m, h][:].rearrange("p j (m t) -> p m j t", t=PACK)
             dst = grouped[m][:, :, h * 64 : (h + 1) * 64, :].rearrange("p t m j -> p m j t")
-            cast(engine, dst, raw[m, h][:].rearrange("p j (m t) -> p m j t", t=PACK))
+            if engine == "V":
+                for a in (0, 2):
+                    cast(engine, dst[:, :, :, a : a + 2], src[:, :, :, a : a + 2])
+            else:
+                cast(engine, dst, src)
 
         def quantize(codes, plane, values):
             nc.vector.quantize_mx(out=codes.bitcast(FP8X4), scales=plane, in_=values)
 
-        def quant_first(m, t=None):
-            if t is None:
-                quantize(wc[m][:], ws[m][:], grouped[m][:].rearrange("p t m j -> p (t m j)"))
-            else:
-                quantize(wc[m][:, t * P : (t + 1) * P], ws[m][:, t * P : (t + 1) * P], grouped[m][:, t].rearrange("p m j -> p (m j)"))
-
-        grouped2 = [keep.tile([P, N, PACK], BF16, name="grp2_%d" % e, align_bytes=64)[:] for e in range(E - 1)]
-        grouped2.append(grouped[2 * E - 1][:, PACK - 1])
-        w2c = [keep.tile([P, N], U32, name="w2c%d" % e, align_bytes=64) for e in range(E)]
+        grouped2 = [keep.tile([P, N, PACK], BF16, name="grp2_%d" % e, align_bytes=64) for e in range(E)]
+        w2c = [placed([P, N], U32, "w2c%d" % e, on_raw(2 * e + 2, 1) if 1 <= e < E - 1 else None) for e in range(E)]
         w2s = [keep.tile([P, N], U8, name="w2s%d" % e, align_bytes=64) for e in range(E)]
 
         def cast_second(e, engine):
-            cast(engine, grouped2[e].rearrange("p (c i) j -> p c j i", i=4), raw2[:, e].rearrange("p j (c i) -> p c j i", i=4))
+            cast(engine, grouped2[e][:].rearrange("p (c i) j -> p c j i", i=4), raw2[e][:].rearrange("p j (c i) -> p c j i", i=4))
 
         def quant_second(e):
-            quantize(w2c[e][:], w2s[e][:], grouped2[e].rearrange("p n j -> p (n j)"))
+            quantize(w2c[e][:], w2s[e][:], grouped2[e][:].rearrange("p n j -> p (n j)"))
 
-        hb_at = {0: on_piece(4, 0), 1: on_piece(6, 0), 2: on_piece(7, 0)}
-        ysb_at = {0: on_piece(6, 0, 2048), 1: on_piece(7, 0, 2048)}
-        hb, ysb, acc, yacc = {}, {}, {}, {}
+        hb, acc, yacc = {}, {}, {}
         hc = [keep.tile([P, C], U32, name="hc%d" % e, align_bytes=64) for e in range(E)]
         hs = [keep.tile([P, C], U8, name="hs%d" % e, align_bytes=64) for e in range(E)]
+        ysb = [keep.tile([P, C], F32, name="ysb%d" % e, align_bytes=64) for e in range(E)]
 
-        def first_layer(e, u):
-            acc[e, u] = hpsum.tile([P, PACK, HALF], F32, name="acc")
-            slots = slice((e % 2) * C + u * HALF, (e % 2) * C + (u + 1) * HALF)
-            for t in range(PACK):
-                for s in range(2):
+        def product(m, tiles=(0, PACK)):
+            e, s = divmod(m, 2)
+            a, b = tiles
+            quantize(wc[m][:, a * P : b * P], ws[m][:, a * P : b * P], grouped[m][:, a:b].rearrange("p t m j -> p (t m j)"))
+            for u in range(2):
+                if s == 0 and a == 0:
+                    acc[e, u] = hpsum.tile([P, PACK, HALF], F32, name="acc")
+                slots = slice((e % 2) * C + u * HALF, (e % 2) * C + (u + 1) * HALF)
+                for t in range(a, b):
                     nc.tensor.matmul_mx(
                         out=acc[e, u][:, t, :],
-                        lhsT=wc[2 * e + s][:, t * P : (t + 1) * P].bitcast(FP8X4),
-                        lhsT_scale=ws[2 * e + s][:, t * P : (t + 1) * P],
+                        lhsT=wc[m][:, t * P : (t + 1) * P].bitcast(FP8X4),
+                        lhsT_scale=ws[m][:, t * P : (t + 1) * P],
                         rhs=words[e // 2, s][:, slots].bitcast(FP8X4),
                         rhs_scale=scales[e // 2, s][:, slots],
-                        start=(s == 0),
-                        stop=(s == 1),
+                        start=(s == 0 and t == 0),
+                        stop=(s == 1 and t == PACK - 1),
                     )
 
-        def relu(e, u):
-            if u == 0:
-                if e in hb_at:
-                    hb[e] = stage.tile([P, C, PACK], BF16, name="hb%d" % e, align_bytes=64, offset=hb_at[e])
-                else:
-                    hb[e] = keep.tile([P, C, PACK], BF16, name="hb%d" % e, align_bytes=64)
-            nc.scalar.activation(hb[e][:, u * HALF : (u + 1) * HALF, :], acc[e, u][:].rearrange("p t n -> p n t"), RELU)
-
-        def quant_hidden(e, a=0, b=C):
-            quantize(hc[e][:, a:b], hs[e][:, a:b], hb[e][:, a:b, :].rearrange("p n t -> p (n t)"))
+        def relu(e, at=None):
+            hb[e] = placed([P, C, PACK], BF16, "hb%d" % e, at)
+            for u in range(2):
+                nc.scalar.activation(hb[e][:, u * HALF : (u + 1) * HALF, :], acc[e, u][:].rearrange("p t n -> p n t"), RELU)
 
         def second_layer(e, a=0, b=C):
-            yacc[e, a] = ypsum.tile([P, b - a], F32, name="yacc")
+            quantize(hc[e][:, a:b], hs[e][:, a:b], hb[e][:, a:b, :].rearrange("p n t -> p (n t)"))
+            if a == 0 or e == E - 1:
+                yacc[e, a] = ypsum.tile([P, C], F32, name="yacc")
+            else:
+                yacc[e, a] = yacc[e, 0]
             nc.tensor.matmul_mx(
-                out=yacc[e, a][:],
+                out=yacc[e, a][:, a:b],
                 lhsT=w2c[e][:].bitcast(FP8X4),
                 lhsT_scale=w2s[e][:],
                 rhs=hc[e][:, a:b].bitcast(FP8X4),
@@ -171,88 +174,52 @@ def tile_moe_duo_relu_kernel(tc, x_words, x_scales, w1, wp, w2, gate, offs, offs
             )
 
         def copy_out(e, a=0, b=C):
-            if a == 0:
-                if e in ysb_at:
-                    ysb[e] = stage.tile([P, C], F32, name="ysb%d" % e, align_bytes=64, offset=ysb_at[e])
-                else:
-                    ysb[e] = keep.tile([P, C], F32, name="ysb%d" % e, align_bytes=64)
-            nc.scalar.copy(ysb[e][:, a:b], yacc[e, a][:])
+            nc.scalar.copy(ysb[e][:, a:b], yacc[e, a][:, a:b])
 
         def scatter(e, a=0, b=C):
             window = out_sb[:].indirect(lists[0][:, (e * C + a) // 16 : (e * C + b) // 16])
             nc.vector.tensor_tensor(window, ysb[e][:, a:b], gate_sb[:, e * C + a : e * C + b], MULT)
 
-        gather(0)
-        gather(1)
-        cast_first(0, 0, "S")
-        cast_first(0, 1, "S")
-        cast_first(1, 0, "S")
-        cast_first(1, 1, "S")
-        cast_first(2, 0, "S")
-        cast_first(2, 1, "S")
-        cast_first(3, 0, "S")
-        quant_first(0)
-        quant_first(1)
-        cast_second(0, "S")
-        quant_first(2)
-        first_layer(0, 0)
-        cast_first(4, 0, "S")
-        cast_first(3, 1, "V")
-        first_layer(0, 1)
-        quant_first(3)
-        relu(0, 0)
-        quant_second(0)
-        cast_first(4, 1, "V")
-        first_layer(1, 0)
-        relu(0, 1)
-        cast_first(5, 0, "S")
-        quant_first(4)
-        first_layer(1, 1)
-        cast_first(5, 1, "V")
-        quant_hidden(0)
-        cast_first(6, 0, "S")
-        quant_first(5)
-        second_layer(0)
-        first_layer(2, 0)
-        cast_first(6, 1, "V")
-        copy_out(0)
-        relu(1, 0)
-        scatter(0)
-        first_layer(2, 1)
-        relu(1, 1)
-        cast_second(1, "S")
-        cast_second(2, "S")
-        quant_first(6)
-        cast_first(7, 0, "S")
-        quant_hidden(1)
-        quant_second(1)
-        quant_second(2)
-        cast_first(7, 1, "V")
-        second_layer(1)
-        relu(2, 0)
-        quant_first(7, 0)
-        quant_first(7, 1)
-        relu(2, 1)
-        quant_first(7, 2)
-        quant_first(7, 3)
-        first_layer(3, 0)
-        cast_second(3, "V")
-        copy_out(1)
-        quant_hidden(2)
-        quant_second(3)
-        first_layer(3, 1)
-        scatter(1)
-        relu(3, 0)
-        second_layer(2)
-        relu(3, 1)
-        quant_hidden(3, 0, HALF)
-        copy_out(2)
-        quant_hidden(3, HALF, C)
-        second_layer(3, 0, HALF)
-        scatter(2)
-        second_layer(3, HALF, C)
-        copy_out(3, 0, HALF)
-        copy_out(3, HALF, C)
-        scatter(3, 0, HALF)
-        scatter(3, HALF, C)
+        def products(m, split):
+            for tiles in (((0, 2), (2, PACK)) if split else ((0, PACK),)):
+                product(m, tiles)
+
+        gather(xs, U8, scales, "gs", 0)
+        gather(xs, U8, scales, "gs", 1)
+        gather(xw, U32, words, "gw", 0)
+        last = E - 1
+        for e in range(E):
+            first, partner = 2 * e, 2 * e + 1
+            cast_first(first, 0, "S")
+            cast_first(first, 1, "S" if e < 2 else "V")
+            if e >= 1:
+                cast_second(e - 1, "S")
+                relu(e - 1, on_raw(first, 1 if e < 2 else 0))
+            if e >= 1:
+                quant_second(e - 1)
+                for u in range(2):
+                    second_layer(e - 1, u * HALF, (u + 1) * HALF)
+                    product(first, (2 * u, 2 * u + 2))
+            else:
+                products(first, False)
+            cast_first(partner, 0, "S")
+            if e >= 1:
+                copy_out(e - 1)
+            cast_first(partner, 1, "S" if e == 0 else "V")
+            products(partner, e > 0)
+            if e == 0:
+                gather(xw, U32, words, "gw", 1, (on_rounded(partner), on_rounded(partner, 2048)))
+            elif e < last:
+                scatter(e - 1)
+        cast_second(last, "S")
+        scatter(last - 1, 0, HALF)
+        relu(last)
+        quant_second(last)
+        second_layer(last, 0, HALF)
+        scatter(last - 1, HALF, C)
+        second_layer(last, HALF, C)
+        copy_out(last, 0, HALF)
+        copy_out(last, HALF, C)
+        scatter(last, 0, HALF)
+        scatter(last, HALF, C)
         nc.sync.dma_start(out, out_sb[:])

@@ -72,6 +72,7 @@ def tile_moe_duo_relu_kernel(tc, x_words, x_scales, w1, wp, w2, gate, offs, offs
         for e in range(E):
             load_first(2 * e, 0)
             if e >= 2:
+                load_gate(e - 2)
                 load_second(e - 1)
             load_first(2 * e, 1)
             if e == 1:
@@ -80,8 +81,6 @@ def tile_moe_duo_relu_kernel(tc, x_words, x_scales, w1, wp, w2, gate, offs, offs
             if e == 0:
                 nc.sync.dma_start(xw[:].bitcast(I32), x_words[0].rearrange("p t d -> p (t d)").bitcast(I32))
             load_first(2 * e + 1, 1)
-            if 1 <= e < E - 1:
-                load_gate(e - 1)
         load_second(E - 1)
         load_gate(E - 2)
         load_gate(E - 1)
@@ -109,11 +108,7 @@ def tile_moe_duo_relu_kernel(tc, x_words, x_scales, w1, wp, w2, gate, offs, offs
         def cast_first(m, h, engine):
             src = raw[m, h][:].rearrange("p j (m t) -> p m j t", t=PACK)
             dst = grouped[m][:, :, h * 64 : (h + 1) * 64, :].rearrange("p t m j -> p m j t")
-            if engine == "V":
-                for a in (0, 2):
-                    cast(engine, dst[:, :, :, a : a + 2], src[:, :, :, a : a + 2])
-            else:
-                cast(engine, dst, src)
+            cast(engine, dst, src)
 
         def quantize(codes, plane, values):
             nc.vector.quantize_mx(out=codes.bitcast(FP8X4), scales=plane, in_=values)
@@ -206,7 +201,7 @@ def tile_moe_duo_relu_kernel(tc, x_words, x_scales, w1, wp, w2, gate, offs, offs
             if e >= 1:
                 copy_out(e - 1)
             cast_first(partner, 1, "S" if e == 0 else "V")
-            products(partner, e > 0)
+            products(partner, e == last)
             if e == 0:
                 gather(xw, U32, words, "gw", 1, (on_rounded(partner), on_rounded(partner, 2048)))
             elif e < last:

@@ -19,7 +19,8 @@ P = 128
 PACK = 4
 HALF = C // 2
 COLS = H // 2
-SLOT_BYTES = PACK * COLS * 4
+SLOT_BYTES = 6144
+cut = [64, 64, 64, 56, 72, 56, 72, 56]
 
 
 def tile_moe_duo_relu_kernel(tc, x_words, x_scales, w1, wp, w2, gate, offs, offs2, out):
@@ -52,10 +53,14 @@ def tile_moe_duo_relu_kernel(tc, x_words, x_scales, w1, wp, w2, gate, offs, offs
 
         raw, raw2 = {}, {}
 
+        def span(m, h):
+            return (0, cut[m]) if h == 0 else (cut[m], P)
+
         def load_first(m, h):
+            a, b = span(m, h)
             rows = (w1, wp)[m % 2][m // 2].rearrange("(p j) c -> p j c", j=PACK)
-            raw[m, h] = placed([P, PACK, COLS], F32, "raw%d%d" % (m, h), on_raw(m, h))
-            nc.sync.dma_start(raw[m, h][:], rows[:, :, h * COLS : (h + 1) * COLS])
+            raw[m, h] = placed([P, PACK, PACK * (b - a)], F32, "raw%d%d" % (m, h), on_raw(m, h))
+            nc.sync.dma_start(raw[m, h][:], rows[:, :, PACK * a : PACK * b])
 
         def load_second(e):
             raw2[e] = placed([P, PACK, N], F32, "raw2_%d" % e, on_raw2(e))
@@ -73,15 +78,12 @@ def tile_moe_duo_relu_kernel(tc, x_words, x_scales, w1, wp, w2, gate, offs, offs
             load_first(2 * e, 0)
             if e >= 2:
                 load_gate(e - 2)
-                load_second(e - 1)
             load_first(2 * e, 1)
-            if e == 1:
-                load_second(e - 1)
-            load_first(2 * e + 1, 0)
             if e == 0:
                 nc.sync.dma_start(xw[:].bitcast(I32), x_words[0].rearrange("p t d -> p (t d)").bitcast(I32))
+            load_first(2 * e + 1, 0)
             load_first(2 * e + 1, 1)
-        load_second(E - 1)
+            load_second(e)
         load_gate(E - 2)
         load_gate(E - 1)
 
@@ -107,14 +109,15 @@ def tile_moe_duo_relu_kernel(tc, x_words, x_scales, w1, wp, w2, gate, offs, offs
 
         def cast_first(m, h, engine):
             src = raw[m, h][:].rearrange("p j (m t) -> p m j t", t=PACK)
-            dst = grouped[m][:, :, h * 64 : (h + 1) * 64, :].rearrange("p t m j -> p m j t")
+            a, b = span(m, h)
+            dst = grouped[m][:, :, a:b, :].rearrange("p t m j -> p m j t")
             cast(engine, dst, src)
 
         def quantize(codes, plane, values):
             nc.vector.quantize_mx(out=codes.bitcast(FP8X4), scales=plane, in_=values)
 
         grouped2 = [keep.tile([P, N, PACK], BF16, name="grp2_%d" % e, align_bytes=64) for e in range(E)]
-        w2c = [placed([P, N], U32, "w2c%d" % e, on_raw(2 * e + 2, 1) if 1 <= e < E - 1 else None) for e in range(E)]
+        w2c = [placed([P, N], U32, "w2c%d" % e, None) for e in range(E)]
         w2s = [keep.tile([P, N], U8, name="w2s%d" % e, align_bytes=64) for e in range(E)]
 
         def cast_second(e, engine):
@@ -126,7 +129,7 @@ def tile_moe_duo_relu_kernel(tc, x_words, x_scales, w1, wp, w2, gate, offs, offs
         hb, acc, yacc = {}, {}, {}
         hc = [keep.tile([P, C], U32, name="hc%d" % e, align_bytes=64) for e in range(E)]
         hs = [keep.tile([P, C], U8, name="hs%d" % e, align_bytes=64) for e in range(E)]
-        ysb = [keep.tile([P, C], F32, name="ysb%d" % e, align_bytes=64) for e in range(E)]
+        ysb = [placed([P, C], F32, "ysb%d" % e, on_raw(2 * e + 3, 0, 1024) if 1 <= e < E - 1 else None) for e in range(E)]
 
         def product(m, tiles=(0, PACK)):
             e, s = divmod(m, 2)
@@ -175,46 +178,59 @@ def tile_moe_duo_relu_kernel(tc, x_words, x_scales, w1, wp, w2, gate, offs, offs
             window = out_sb[:].indirect(lists[0][:, (e * C + a) // 16 : (e * C + b) // 16])
             nc.vector.tensor_tensor(window, ysb[e][:, a:b], gate_sb[:, e * C + a : e * C + b], MULT)
 
-        def products(m, split):
-            for tiles in (((0, 2), (2, PACK)) if split else ((0, PACK),)):
-                product(m, tiles)
+        def products(m):
+            product(m, (0, 2))
+            product(m, (2, PACK))
 
-        gather(xs, U8, scales, "gs", 0)
-        gather(xs, U8, scales, "gs", 1)
-        gather(xw, U32, words, "gw", 0)
+        for pair in range(2):
+            gather(xs, U8, scales, "gs", pair)
+        for pair in range(2):
+            gather(xw, U32, words, "gw", pair)
         last = E - 1
-        for e in range(E):
+        for m in range(3):
+            cast_first(m, 0, "S")
+            cast_first(m, 1, "S")
+            product(m)
+            if m == 1:
+                cast_second(0, "S")
+        cast_first(3, 0, "S")
+        quant_second(0)
+        cast_first(3, 1, "V")
+        relu(0, on_raw(3, 0))
+        products(3)
+        cast_second(1, "S")
+        second_layer(0)
+        copy_out(0)
+        for e in range(2, E):
             first, partner = 2 * e, 2 * e + 1
-            cast_first(first, 0, "S")
-            cast_first(first, 1, "S" if e < 2 else "V")
-            if e >= 1:
-                cast_second(e - 1, "S")
-                relu(e - 1, on_raw(first, 1 if e < 2 else 0))
-            if e >= 1:
-                quant_second(e - 1)
-                for u in range(2):
-                    second_layer(e - 1, u * HALF, (u + 1) * HALF)
-                    product(first, (2 * u, 2 * u + 2))
+            cast_first(first, 0, "V")
+            quant_second(e - 1)
+            if e == last:
+                cast_first(first, 1, "S")
+                scatter(e - 2)
+                product(first)
+                relu(e - 1, on_raw(first, 1))
+                cast_first(partner, 0, "S")
+                cast_first(partner, 1, "V")
+                second_layer(e - 1)
             else:
-                products(first, False)
-            cast_first(partner, 0, "S")
-            if e >= 1:
-                copy_out(e - 1)
-            cast_first(partner, 1, "S" if e == 0 else "V")
-            products(partner, e == last)
-            if e == 0:
-                gather(xw, U32, words, "gw", 1, (on_rounded(partner), on_rounded(partner, 2048)))
-            elif e < last:
-                scatter(e - 1)
-        cast_second(last, "S")
-        scatter(last - 1, 0, HALF)
-        relu(last)
+                relu(e - 1)
+                scatter(e - 2)
+                second_layer(e - 1)
+                cast_first(first, 1, "S")
+                product(first)
+                cast_first(partner, 0, "S")
+                cast_first(partner, 1, "V")
+            copy_out(e - 1)
+            products(partner)
+            cast_second(e, "S")
         quant_second(last)
+        relu(last)
+        scatter(last - 1, 0, HALF)
         second_layer(last, 0, HALF)
-        scatter(last - 1, HALF, C)
         second_layer(last, HALF, C)
         copy_out(last, 0, HALF)
+        scatter(last - 1, HALF, C)
         copy_out(last, HALF, C)
-        scatter(last, 0, HALF)
-        scatter(last, HALF, C)
+        scatter(last)
         nc.sync.dma_start(out, out_sb[:])

@@ -17,10 +17,11 @@ MULT = mybir.AluOpType.mult
 
 P = 128
 PACK = 4
+LIST_ROWS = 16
 HALF = C // 2
 COLS = H // 2
-SLOT_BYTES = 6144
-cut = [64, 64, 64, 56, 72, 56, 72, 56]
+MATRICES = 2 * E
+AREA = PACK * COLS * 4
 
 
 def tile_moe_duo_relu_kernel(tc, x_words, x_scales, w1, wp, w2, gate, offs, offs2, out):
@@ -31,206 +32,188 @@ def tile_moe_duo_relu_kernel(tc, x_words, x_scales, w1, wp, w2, gate, offs, offs
         hpsum = ctx.enter_context(tc.psum_pool(name="hpsum", bufs=6))
         ypsum = ctx.enter_context(tc.psum_pool(name="ypsum", bufs=2))
 
-        lists = [keep.tile([P, T // 16], U16, name="offs_sb"), keep.tile([P, T // 16], U16, name="offs2_sb")]
+        lists = [keep.tile([P, T // LIST_ROWS], U16, name="offs_sb"), keep.tile([P, T // LIST_ROWS], U16, name="offs2_sb")]
         xw = keep.tile([P, T], U32, name="xw", align_bytes=64)
         xs = keep.tile([P, T], U8, name="xs", align_bytes=64)
         gate_sb = keep.tile([P, E * C], F32, name="gate_sb", align_bytes=64)
         out_sb = keep.tile([P, T], F32, name="out_sb", align_bytes=64)
 
-        def on_raw(m, h, skip=0):
-            return (2 * m + h) * SLOT_BYTES + skip
+        def piece_area(m, piece):
+            return (2 * m + piece) * AREA
 
-        def on_rounded(m, skip=0):
-            return (4 * E + m) * SLOT_BYTES + skip
+        def rounded_area(m):
+            return (2 * MATRICES + m) * AREA
 
-        def on_raw2(e):
-            return (6 * E + e) * SLOT_BYTES
+        def second_area(e):
+            return (3 * MATRICES + e) * AREA
 
-        def placed(shape, dtype, name, at):
+        def codes_area(e):
+            return (3 * MATRICES + E + e) * AREA
+
+        def placed(shape, dtype, name, at=None):
             if at is None:
                 return keep.tile(shape, dtype, name=name, align_bytes=64)
             return stage.tile(shape, dtype, name=name, align_bytes=64, offset=at)
 
         raw, raw2 = {}, {}
 
-        def span(m, h):
-            return (0, cut[m]) if h == 0 else (cut[m], P)
-
-        def load_first(m, h):
-            a, b = span(m, h)
+        def load_first(m, piece):
             rows = (w1, wp)[m % 2][m // 2].rearrange("(p j) c -> p j c", j=PACK)
-            raw[m, h] = placed([P, PACK, PACK * (b - a)], F32, "raw%d%d" % (m, h), on_raw(m, h))
-            nc.sync.dma_start(raw[m, h][:], rows[:, :, PACK * a : PACK * b])
+            raw[m, piece] = placed([P, PACK, COLS], F32, "raw%d%d" % (m, piece), piece_area(m, piece))
+            nc.sync.dma_start(raw[m, piece][:], rows[:, :, piece * COLS : (piece + 1) * COLS])
 
         def load_second(e):
-            raw2[e] = placed([P, PACK, N], F32, "raw2_%d" % e, on_raw2(e))
+            raw2[e] = placed([P, PACK, N], F32, "raw2_%d" % e, second_area(e))
             nc.sync.dma_start(raw2[e][:], w2[e].rearrange("(p j) n -> p j n", j=PACK))
 
-        def load_gate(e):
-            nc.sync.dma_start(gate_sb[:, e * C : (e + 1) * C], gate[:, e * C : (e + 1) * C])
+        def load_gate(first, end):
+            nc.sync.dma_start(gate_sb[:, first * C : end * C], gate[:, first * C : end * C])
 
         nc.sync.dma_start(lists[0][:], offs)
         for q in range(4):
             rows = x_scales[0, 4 * q : 4 * q + 4, :].bitcast(I32)
             nc.sync.dma_start(xs[32 * q : 32 * q + 32, :].bitcast(I32), rows.partition_broadcast(8))
         nc.sync.dma_start(lists[1][:], offs2)
-        for e in range(E):
-            load_first(2 * e, 0)
-            if e >= 2:
-                load_gate(e - 2)
-            load_first(2 * e, 1)
-            if e == 0:
+        for m in range(MATRICES):
+            load_first(m, 0)
+            if m == 4:
+                load_gate(0, 1)
+            load_first(m, 1)
+            if m == 0:
                 nc.sync.dma_start(xw[:].bitcast(I32), x_words[0].rearrange("p t d -> p (t d)").bitcast(I32))
-            load_first(2 * e + 1, 0)
-            load_first(2 * e + 1, 1)
-            load_second(e)
-        load_gate(E - 2)
-        load_gate(E - 1)
+            if m in (1, 3):
+                load_second(m // 2)
+        load_second(2)
+        load_second(3)
+        load_gate(1, E)
 
         words, scales = {}, {}
 
-        def gather(table, dtype, into, label, pair, at=(None, None)):
-            cols = slice(pair * 2 * C // 16, (pair + 1) * 2 * C // 16)
-            for s in range(2):
-                into[pair, s] = placed([P, 2 * C], dtype, "%s%d%d" % (label, pair, s), at[s])
-                nc.vector.tensor_copy(into[pair, s][:], table[:].indirect(lists[s][:, cols]))
+        def gather(table, dtype, into, label):
+            for pair in range(E // 2):
+                cols = slice(pair * 2 * C // LIST_ROWS, (pair + 1) * 2 * C // LIST_ROWS)
+                for side in range(2):
+                    into[pair, side] = placed([P, 2 * C], dtype, "%s%d%d" % (label, pair, side))
+                    nc.vector.tensor_copy(into[pair, side][:], table[:].indirect(lists[side][:, cols]))
 
-        grouped = [placed([P, PACK, P, PACK], BF16, "grp%d" % m, on_rounded(m)) for m in range(2 * E)]
-        wc = [keep.tile([P, H], U32, name="wc%d" % m, align_bytes=64) for m in range(2 * E)]
-        ws = [keep.tile([P, H], U8, name="ws%d" % m, align_bytes=64) for m in range(2 * E)]
+        rounded = [placed([P, PACK, P, PACK], BF16, "grp%d" % m, rounded_area(m)) for m in range(MATRICES)]
+        rounded2 = [placed([P, N, PACK], BF16, "grp2_%d" % e) for e in range(E)]
+        wc, ws, w2c, w2s, hb, hc, hs, ysb, acc, yacc = {}, {}, {}, {}, {}, {}, {}, {}, {}, {}
 
-        def cast(engine, dst, src):
-            if engine == "G":
-                nc.gpsimd.tensor_copy(dst, src)
-            elif engine == "V":
-                nc.vector.tensor_copy(dst, src)
-            else:
-                nc.scalar.copy(dst, src)
+        def round_first(m, piece, copy):
+            src = raw[m, piece][:].rearrange("p j (q t) -> p q j t", t=PACK)
+            groups = slice(piece * COLS // PACK, (piece + 1) * COLS // PACK)
+            copy(rounded[m][:, :, groups, :].rearrange("p t q j -> p q j t"), src)
 
-        def cast_first(m, h, engine):
-            src = raw[m, h][:].rearrange("p j (m t) -> p m j t", t=PACK)
-            a, b = span(m, h)
-            dst = grouped[m][:, :, a:b, :].rearrange("p t m j -> p m j t")
-            cast(engine, dst, src)
+        def round_second(e, copy):
+            copy(rounded2[e][:].rearrange("p (c i) j -> p c j i", i=4), raw2[e][:].rearrange("p j (c i) -> p c j i", i=4))
 
         def quantize(codes, plane, values):
             nc.vector.quantize_mx(out=codes.bitcast(FP8X4), scales=plane, in_=values)
 
-        grouped2 = [keep.tile([P, N, PACK], BF16, name="grp2_%d" % e, align_bytes=64) for e in range(E)]
-        w2c = [placed([P, N], U32, "w2c%d" % e, None) for e in range(E)]
-        w2s = [keep.tile([P, N], U8, name="w2s%d" % e, align_bytes=64) for e in range(E)]
+        def quantize_second(e):
+            w2c[e] = placed([P, N], U32, "w2c%d" % e)
+            w2s[e] = placed([P, N], U8, "w2s%d" % e)
+            quantize(w2c[e][:], w2s[e][:], rounded2[e][:].rearrange("p n j -> p (n j)"))
 
-        def cast_second(e, engine):
-            cast(engine, grouped2[e][:].rearrange("p (c i) j -> p c j i", i=4), raw2[e][:].rearrange("p j (c i) -> p c j i", i=4))
-
-        def quant_second(e):
-            quantize(w2c[e][:], w2s[e][:], grouped2[e][:].rearrange("p n j -> p (n j)"))
-
-        hb, acc, yacc = {}, {}, {}
-        hc = [keep.tile([P, C], U32, name="hc%d" % e, align_bytes=64) for e in range(E)]
-        hs = [keep.tile([P, C], U8, name="hs%d" % e, align_bytes=64) for e in range(E)]
-        ysb = [placed([P, C], F32, "ysb%d" % e, on_raw(2 * e + 3, 0, 1024) if 1 <= e < E - 1 else None) for e in range(E)]
-
-        def product(m, tiles=(0, PACK)):
-            e, s = divmod(m, 2)
-            a, b = tiles
-            quantize(wc[m][:, a * P : b * P], ws[m][:, a * P : b * P], grouped[m][:, a:b].rearrange("p t m j -> p (t m j)"))
-            for u in range(2):
-                if s == 0 and a == 0:
+        def first_layer(m, parts=1, at=None):
+            e, side = divmod(m, 2)
+            wc[m] = placed([P, H], U32, "wc%d" % m, at)
+            ws[m] = placed([P, H], U8, "ws%d" % m)
+            if side == 0:
+                for u in range(2):
                     acc[e, u] = hpsum.tile([P, PACK, HALF], F32, name="acc")
-                slots = slice((e % 2) * C + u * HALF, (e % 2) * C + (u + 1) * HALF)
-                for t in range(a, b):
-                    nc.tensor.matmul_mx(
-                        out=acc[e, u][:, t, :],
-                        lhsT=wc[m][:, t * P : (t + 1) * P].bitcast(FP8X4),
-                        lhsT_scale=ws[m][:, t * P : (t + 1) * P],
-                        rhs=words[e // 2, s][:, slots].bitcast(FP8X4),
-                        rhs_scale=scales[e // 2, s][:, slots],
-                        start=(s == 0 and t == 0),
-                        stop=(s == 1 and t == PACK - 1),
-                    )
+            for a in range(0, PACK, PACK // parts):
+                b = a + PACK // parts
+                quantize(wc[m][:, a * P : b * P], ws[m][:, a * P : b * P], rounded[m][:, a:b].rearrange("p t q j -> p (t q j)"))
+                for u in range(2):
+                    slots = slice((e % 2) * C + u * HALF, (e % 2) * C + (u + 1) * HALF)
+                    for t in range(a, b):
+                        nc.tensor.matmul_mx(
+                            out=acc[e, u][:, t, :],
+                            lhsT=wc[m][:, t * P : (t + 1) * P].bitcast(FP8X4),
+                            lhsT_scale=ws[m][:, t * P : (t + 1) * P],
+                            rhs=words[e // 2, side][:, slots].bitcast(FP8X4),
+                            rhs_scale=scales[e // 2, side][:, slots],
+                            start=(side == 0 and t == 0),
+                            stop=(side == 1 and t == PACK - 1),
+                        )
 
         def relu(e, at=None):
             hb[e] = placed([P, C, PACK], BF16, "hb%d" % e, at)
             for u in range(2):
                 nc.scalar.activation(hb[e][:, u * HALF : (u + 1) * HALF, :], acc[e, u][:].rearrange("p t n -> p n t"), RELU)
 
-        def second_layer(e, a=0, b=C):
-            quantize(hc[e][:, a:b], hs[e][:, a:b], hb[e][:, a:b, :].rearrange("p n t -> p (n t)"))
-            if a == 0 or e == E - 1:
-                yacc[e, a] = ypsum.tile([P, C], F32, name="yacc")
-            else:
-                yacc[e, a] = yacc[e, 0]
+        def second_layer(e, at=None):
+            hc[e] = placed([P, C], U32, "hc%d" % e, at)
+            hs[e] = placed([P, C], U8, "hs%d" % e)
+            quantize(hc[e][:], hs[e][:], hb[e][:].rearrange("p n t -> p (n t)"))
+            yacc[e] = ypsum.tile([P, C], F32, name="yacc")
             nc.tensor.matmul_mx(
-                out=yacc[e, a][:, a:b],
+                out=yacc[e][:],
                 lhsT=w2c[e][:].bitcast(FP8X4),
                 lhsT_scale=w2s[e][:],
-                rhs=hc[e][:, a:b].bitcast(FP8X4),
-                rhs_scale=hs[e][:, a:b],
+                rhs=hc[e][:].bitcast(FP8X4),
+                rhs_scale=hs[e][:],
                 start=True,
                 stop=True,
             )
 
-        def copy_out(e, a=0, b=C):
-            nc.scalar.copy(ysb[e][:, a:b], yacc[e, a][:, a:b])
+        def copy_out(e):
+            ysb[e] = placed([P, C], F32, "ysb%d" % e)
+            nc.scalar.copy(ysb[e][:], yacc[e][:])
 
         def scatter(e, a=0, b=C):
-            window = out_sb[:].indirect(lists[0][:, (e * C + a) // 16 : (e * C + b) // 16])
+            window = out_sb[:].indirect(lists[0][:, (e * C + a) // LIST_ROWS : (e * C + b) // LIST_ROWS])
             nc.vector.tensor_tensor(window, ysb[e][:, a:b], gate_sb[:, e * C + a : e * C + b], MULT)
 
-        def products(m):
-            product(m, (0, 2))
-            product(m, (2, PACK))
+        on_scalar, on_vector = nc.scalar.copy, nc.vector.tensor_copy
 
-        for pair in range(2):
-            gather(xs, U8, scales, "gs", pair)
-        for pair in range(2):
-            gather(xw, U32, words, "gw", pair)
-        last = E - 1
+        gather(xs, U8, scales, "gs")
+        gather(xw, U32, words, "gw")
         for m in range(3):
-            cast_first(m, 0, "S")
-            cast_first(m, 1, "S")
-            product(m)
+            round_first(m, 0, on_scalar)
+            round_first(m, 1, on_scalar)
+            first_layer(m)
             if m == 1:
-                cast_second(0, "S")
-        cast_first(3, 0, "S")
-        quant_second(0)
-        cast_first(3, 1, "V")
-        relu(0, on_raw(3, 0))
-        products(3)
-        cast_second(1, "S")
-        second_layer(0)
+                round_second(0, on_scalar)
+                quantize_second(0)
+        round_first(3, 0, on_scalar)
+        round_first(3, 1, on_vector)
+        first_layer(3, parts=2)
+        round_second(1, on_scalar)
+        relu(0, second_area(1))
+        quantize_second(1)
+        second_layer(0, codes_area(0))
+        round_first(4, 0, on_scalar)
+        round_first(4, 1, on_vector)
         copy_out(0)
-        for e in range(2, E):
-            first, partner = 2 * e, 2 * e + 1
-            cast_first(first, 0, "V")
-            quant_second(e - 1)
-            if e == last:
-                cast_first(first, 1, "S")
-                scatter(e - 2)
-                product(first)
-                relu(e - 1, on_raw(first, 1))
-                cast_first(partner, 0, "S")
-                cast_first(partner, 1, "V")
-                second_layer(e - 1)
-            else:
-                relu(e - 1)
-                scatter(e - 2)
-                second_layer(e - 1)
-                cast_first(first, 1, "S")
-                product(first)
-                cast_first(partner, 0, "S")
-                cast_first(partner, 1, "V")
-            copy_out(e - 1)
-            products(partner)
-            cast_second(e, "S")
-        quant_second(last)
-        relu(last)
-        scatter(last - 1, 0, HALF)
-        second_layer(last, 0, HALF)
-        second_layer(last, HALF, C)
-        copy_out(last, 0, HALF)
-        scatter(last - 1, HALF, C)
-        copy_out(last, HALF, C)
-        scatter(last)
+        relu(1, codes_area(0))
+        scatter(0)
+        second_layer(1)
+        round_first(5, 0, on_scalar)
+        round_first(5, 1, on_vector)
+        copy_out(1)
+        first_layer(4, at=piece_area(5, 1))
+        first_layer(5)
+        round_first(6, 0, on_scalar)
+        round_first(6, 1, on_vector)
+        first_layer(6)
+        round_first(7, 0, on_scalar)
+        round_first(7, 1, on_vector)
+        relu(2, piece_area(7, 0))
+        round_second(2, on_vector)
+        first_layer(7, parts=2)
+        round_second(3, on_scalar)
+        quantize_second(2)
+        second_layer(2, rounded_area(7))
+        quantize_second(3)
+        relu(3)
+        copy_out(2)
+        scatter(1)
+        second_layer(3)
+        scatter(2, 0, HALF)
+        scatter(2, HALF, C)
+        copy_out(3)
+        scatter(3)
         nc.sync.dma_start(out, out_sb[:])

@@ -22,6 +22,8 @@ HALF = C // 2
 COLS = H // 2
 MATRICES = 2 * E
 AREA = PACK * COLS * 4
+FIRST_SCATTER_AT = 5
+HIDDEN_BYTES = C * PACK * 2
 
 
 def tile_moe_duo_relu_kernel(tc, x_words, x_scales, w1, wp, w2, gate, offs, offs2, out):
@@ -41,14 +43,8 @@ def tile_moe_duo_relu_kernel(tc, x_words, x_scales, w1, wp, w2, gate, offs, offs
         def piece_area(m, piece):
             return (2 * m + piece) * AREA
 
-        def rounded_area(m):
-            return (2 * MATRICES + m) * AREA
-
         def second_area(e):
-            return (3 * MATRICES + e) * AREA
-
-        def codes_area(e):
-            return (3 * MATRICES + E + e) * AREA
+            return (2 * MATRICES + e) * AREA
 
         def placed(shape, dtype, name, at=None):
             if at is None:
@@ -76,11 +72,11 @@ def tile_moe_duo_relu_kernel(tc, x_words, x_scales, w1, wp, w2, gate, offs, offs
         nc.sync.dma_start(lists[1][:], offs2)
         for m in range(MATRICES):
             load_first(m, 0)
-            if m == 4:
-                load_gate(0, 1)
-            load_first(m, 1)
             if m == 0:
                 nc.sync.dma_start(xw[:].bitcast(I32), x_words[0].rearrange("p t d -> p (t d)").bitcast(I32))
+            load_first(m, 1)
+            if m == FIRST_SCATTER_AT:
+                load_gate(0, 1)
             if m in (1, 3):
                 load_second(m // 2)
         load_second(2)
@@ -96,9 +92,13 @@ def tile_moe_duo_relu_kernel(tc, x_words, x_scales, w1, wp, w2, gate, offs, offs
                     into[pair, side] = placed([P, 2 * C], dtype, "%s%d%d" % (label, pair, side))
                     nc.vector.tensor_copy(into[pair, side][:], table[:].indirect(lists[side][:, cols]))
 
-        rounded = [placed([P, PACK, P, PACK], BF16, "grp%d" % m, rounded_area(m)) for m in range(MATRICES)]
-        rounded2 = [placed([P, N, PACK], BF16, "grp2_%d" % e) for e in range(E)]
-        wc, ws, w2c, w2s, hb, hc, hs, ysb, acc, yacc = {}, {}, {}, {}, {}, {}, {}, {}, {}, {}
+        def tiles(count, shape, dtype, label):
+            return [placed(shape, dtype, "%s%d" % (label, i)) for i in range(count)]
+
+        rounded, wc, ws = tiles(MATRICES, [P, PACK, P, PACK], BF16, "grp"), tiles(MATRICES, [P, H], U32, "wc"), tiles(MATRICES, [P, H], U8, "ws")
+        rounded2, w2c, w2s = tiles(E, [P, N, PACK], BF16, "grp2_"), tiles(E, [P, N], U32, "w2c"), tiles(E, [P, N], U8, "w2s")
+        hc, hs = tiles(E, [P, C], U32, "hc"), tiles(E, [P, C], U8, "hs")
+        hb, ysb, acc, yacc = {}, {}, {}, {}
 
         def round_first(m, piece, copy):
             src = raw[m, piece][:].rearrange("p j (q t) -> p q j t", t=PACK)
@@ -112,31 +112,28 @@ def tile_moe_duo_relu_kernel(tc, x_words, x_scales, w1, wp, w2, gate, offs, offs
             nc.vector.quantize_mx(out=codes.bitcast(FP8X4), scales=plane, in_=values)
 
         def quantize_second(e):
-            w2c[e] = placed([P, N], U32, "w2c%d" % e)
-            w2s[e] = placed([P, N], U8, "w2s%d" % e)
             quantize(w2c[e][:], w2s[e][:], rounded2[e][:].rearrange("p n j -> p (n j)"))
 
-        def first_layer(m, parts=1, at=None):
-            e, side = divmod(m, 2)
-            wc[m] = placed([P, H], U32, "wc%d" % m, at)
-            ws[m] = placed([P, H], U8, "ws%d" % m)
-            if side == 0:
-                for u in range(2):
-                    acc[e, u] = hpsum.tile([P, PACK, HALF], F32, name="acc")
+        def quantize_first(m, parts=1):
             for a in range(0, PACK, PACK // parts):
                 b = a + PACK // parts
                 quantize(wc[m][:, a * P : b * P], ws[m][:, a * P : b * P], rounded[m][:, a:b].rearrange("p t q j -> p (t q j)"))
-                for u in range(2):
-                    slots = slice((e % 2) * C + u * HALF, (e % 2) * C + (u + 1) * HALF)
-                    for t in range(a, b):
+
+        def first_layer(e):
+            for u in range(2):
+                acc[e, u] = hpsum.tile([P, PACK, HALF], F32, name="acc")
+                slots = slice((e % 2) * C + u * HALF, (e % 2) * C + (u + 1) * HALF)
+                for t in range(PACK):
+                    for side in range(2):
+                        m = 2 * e + side
                         nc.tensor.matmul_mx(
                             out=acc[e, u][:, t, :],
                             lhsT=wc[m][:, t * P : (t + 1) * P].bitcast(FP8X4),
                             lhsT_scale=ws[m][:, t * P : (t + 1) * P],
                             rhs=words[e // 2, side][:, slots].bitcast(FP8X4),
                             rhs_scale=scales[e // 2, side][:, slots],
-                            start=(side == 0 and t == 0),
-                            stop=(side == 1 and t == PACK - 1),
+                            start=(side == 0),
+                            stop=(side == 1),
                         )
 
         def relu(e, at=None):
@@ -144,9 +141,7 @@ def tile_moe_duo_relu_kernel(tc, x_words, x_scales, w1, wp, w2, gate, offs, offs
             for u in range(2):
                 nc.scalar.activation(hb[e][:, u * HALF : (u + 1) * HALF, :], acc[e, u][:].rearrange("p t n -> p n t"), RELU)
 
-        def second_layer(e, at=None):
-            hc[e] = placed([P, C], U32, "hc%d" % e, at)
-            hs[e] = placed([P, C], U8, "hs%d" % e)
+        def second_layer(e):
             quantize(hc[e][:], hs[e][:], hb[e][:].rearrange("p n t -> p (n t)"))
             yacc[e] = ypsum.tile([P, C], F32, name="yacc")
             nc.tensor.matmul_mx(
@@ -159,8 +154,8 @@ def tile_moe_duo_relu_kernel(tc, x_words, x_scales, w1, wp, w2, gate, offs, offs
                 stop=True,
             )
 
-        def copy_out(e):
-            ysb[e] = placed([P, C], F32, "ysb%d" % e)
+        def copy_out(e, at=None):
+            ysb[e] = placed([P, C], F32, "ysb%d" % e, at)
             nc.scalar.copy(ysb[e][:], yacc[e][:])
 
         def scatter(e, a=0, b=C):
@@ -169,48 +164,57 @@ def tile_moe_duo_relu_kernel(tc, x_words, x_scales, w1, wp, w2, gate, offs, offs
 
         on_scalar, on_vector = nc.scalar.copy, nc.vector.tensor_copy
 
+        def round_shared(m):
+            round_first(m, 0, on_scalar)
+            round_first(m, 1, on_vector)
+
         gather(xs, U8, scales, "gs")
         gather(xw, U32, words, "gw")
         for m in range(3):
             round_first(m, 0, on_scalar)
             round_first(m, 1, on_scalar)
-            first_layer(m)
+            quantize_first(m)
             if m == 1:
+                first_layer(0)
                 round_second(0, on_scalar)
                 quantize_second(0)
-        round_first(3, 0, on_scalar)
-        round_first(3, 1, on_vector)
-        first_layer(3, parts=2)
+
+        round_shared(3)
         round_second(1, on_scalar)
-        relu(0, second_area(1))
+        quantize_first(3)
+        first_layer(1)
         quantize_second(1)
-        second_layer(0, codes_area(0))
-        round_first(4, 0, on_scalar)
-        round_first(4, 1, on_vector)
-        copy_out(0)
-        relu(1, codes_area(0))
+
+        round_shared(4)
+        relu(0, piece_area(4, 0))
+        quantize_first(4)
+        second_layer(0)
+
+        round_shared(FIRST_SCATTER_AT)
+        copy_out(0, piece_area(FIRST_SCATTER_AT, 0) + HIDDEN_BYTES)
+        relu(1, piece_area(FIRST_SCATTER_AT, 0))
         scatter(0)
+        quantize_first(FIRST_SCATTER_AT)
+        first_layer(2)
+
+        round_shared(6)
         second_layer(1)
-        round_first(5, 0, on_scalar)
-        round_first(5, 1, on_vector)
-        copy_out(1)
-        first_layer(4, at=piece_area(5, 1))
-        first_layer(5)
-        round_first(6, 0, on_scalar)
-        round_first(6, 1, on_vector)
-        first_layer(6)
-        round_first(7, 0, on_scalar)
-        round_first(7, 1, on_vector)
+        quantize_first(6)
+
+        round_shared(7)
         relu(2, piece_area(7, 0))
+        copy_out(1, piece_area(7, 0) + HIDDEN_BYTES)
         round_second(2, on_vector)
-        first_layer(7, parts=2)
-        round_second(3, on_scalar)
+        quantize_first(7, parts=PACK)
+        first_layer(3)
         quantize_second(2)
-        second_layer(2, rounded_area(7))
+        second_layer(2)
+        round_second(3, on_scalar)
+
+        scatter(1)
         quantize_second(3)
         relu(3)
         copy_out(2)
-        scatter(1)
         second_layer(3)
         scatter(2, 0, HALF)
         scatter(2, HALF, C)

@@ -63,7 +63,7 @@ def tile_moe_duo_relu_kernel(tc, x_words, x_scales, w1, wp, w2, gate, offs, offs
             nc.sync.dma_start(raw2[e][:], w2[e].rearrange("(p j) n -> p j n", j=PACK))
 
         def load_gate(first, end):
-            nc.sync.dma_start(gate_sb[:, first * C : end * C], gate[:, first * C : end * C])
+            nc.sync.dma_start(gate_sb[:, first * HALF : end * HALF], gate[:, first * HALF : end * HALF])
 
         nc.sync.dma_start(lists[0][:], offs)
         for q in range(4):
@@ -76,12 +76,12 @@ def tile_moe_duo_relu_kernel(tc, x_words, x_scales, w1, wp, w2, gate, offs, offs
                 nc.sync.dma_start(xw[:].bitcast(I32), x_words[0].rearrange("p t d -> p (t d)").bitcast(I32))
             load_first(m, 1)
             if m == FIRST_SCATTER_AT:
-                load_gate(0, 1)
+                load_gate(0, 2)
             if m in (1, 3):
                 load_second(m // 2)
         load_second(2)
         load_second(3)
-        load_gate(1, E)
+        load_gate(2, 8)
 
         words, scales = {}, {}
 
@@ -100,10 +100,12 @@ def tile_moe_duo_relu_kernel(tc, x_words, x_scales, w1, wp, w2, gate, offs, offs
         hc, hs = tiles(E, [P, C], U32, "hc"), tiles(E, [P, C], U8, "hs")
         hb, ysb, acc, yacc = {}, {}, {}, {}
 
-        def round_first(m, piece, copy):
+        def round_first(m, piece, copy, parts=1):
             src = raw[m, piece][:].rearrange("p j (q t) -> p q j t", t=PACK)
             groups = slice(piece * COLS // PACK, (piece + 1) * COLS // PACK)
-            copy(rounded[m][:, :, groups, :].rearrange("p t q j -> p q j t"), src)
+            for a in range(0, PACK, PACK // parts):
+                b = a + PACK // parts
+                copy(rounded[m][:, a:b, groups, :].rearrange("p t q j -> p q j t"), src[:, :, :, a:b])
 
         def round_second(e, copy):
             copy(rounded2[e][:].rearrange("p (c i) j -> p c j i", i=4), raw2[e][:].rearrange("p j (c i) -> p c j i", i=4))
@@ -119,54 +121,57 @@ def tile_moe_duo_relu_kernel(tc, x_words, x_scales, w1, wp, w2, gate, offs, offs
                 b = a + PACK // parts
                 quantize(wc[m][:, a * P : b * P], ws[m][:, a * P : b * P], rounded[m][:, a:b].rearrange("p t q j -> p (t q j)"))
 
-        def first_layer(e):
-            for u in range(2):
-                acc[e, u] = hpsum.tile([P, PACK, HALF], F32, name="acc")
-                slots = slice((e % 2) * C + u * HALF, (e % 2) * C + (u + 1) * HALF)
-                for t in range(PACK):
-                    for side in range(2):
-                        m = 2 * e + side
-                        nc.tensor.matmul_mx(
-                            out=acc[e, u][:, t, :],
-                            lhsT=wc[m][:, t * P : (t + 1) * P].bitcast(FP8X4),
-                            lhsT_scale=ws[m][:, t * P : (t + 1) * P],
-                            rhs=words[e // 2, side][:, slots].bitcast(FP8X4),
-                            rhs_scale=scales[e // 2, side][:, slots],
-                            start=(side == 0),
-                            stop=(side == 1),
-                        )
+        def first_layer(m):
+            e, side = divmod(m, 2)
+            if side == 0:
+                for u in range(2):
+                    acc[e, u] = hpsum.tile([P, PACK, HALF], F32, name="acc")
+            for t in range(PACK):
+                for u in range(2):
+                    slots = slice((e % 2) * C + u * HALF, (e % 2) * C + (u + 1) * HALF)
+                    nc.tensor.matmul_mx(
+                        out=acc[e, u][:, t, :],
+                        lhsT=wc[m][:, t * P : (t + 1) * P].bitcast(FP8X4),
+                        lhsT_scale=ws[m][:, t * P : (t + 1) * P],
+                        rhs=words[e // 2, side][:, slots].bitcast(FP8X4),
+                        rhs_scale=scales[e // 2, side][:, slots],
+                        start=(side == 0 and t == 0),
+                        stop=(side == 1 and t == PACK - 1),
+                    )
 
-        def relu(e, at=None):
-            hb[e] = placed([P, C, PACK], BF16, "hb%d" % e, at)
-            for u in range(2):
-                nc.scalar.activation(hb[e][:, u * HALF : (u + 1) * HALF, :], acc[e, u][:].rearrange("p t n -> p n t"), RELU)
+        def relu(e, at=None, a=0, b=C):
+            hb[e, a] = placed([P, b - a, PACK], BF16, "hb%d_%d" % (e, a), at)
+            for u in range(a, b, HALF):
+                nc.scalar.activation(hb[e, a][:, u - a : u - a + HALF, :], acc[e, u // HALF][:].rearrange("p t n -> p n t"), RELU)
 
-        def second_layer(e):
-            quantize(hc[e][:], hs[e][:], hb[e][:].rearrange("p n t -> p (n t)"))
-            yacc[e] = ypsum.tile([P, C], F32, name="yacc")
+        def second_layer(e, a=0, b=C):
+            quantize(hc[e][:, a:b], hs[e][:, a:b], hb[e, a][:].rearrange("p n t -> p (n t)"))
+            sums = ypsum.tile([P, b - a], F32, name="yacc")
+            for u in range(a, b, HALF):
+                yacc[e, u] = (sums, u - a)
             nc.tensor.matmul_mx(
-                out=yacc[e][:],
+                out=sums[:],
                 lhsT=w2c[e][:].bitcast(FP8X4),
                 lhsT_scale=w2s[e][:],
-                rhs=hc[e][:].bitcast(FP8X4),
-                rhs_scale=hs[e][:],
+                rhs=hc[e][:, a:b].bitcast(FP8X4),
+                rhs_scale=hs[e][:, a:b],
                 start=True,
                 stop=True,
             )
 
-        def copy_out(e, at=None):
-            ysb[e] = placed([P, C], F32, "ysb%d" % e, at)
-            nc.scalar.copy(ysb[e][:], yacc[e][:])
+        def copy_out(e, a=0, b=C, at=None):
+            results = placed([P, b - a], F32, "ysb%d_%d" % (e, a), at)
+            for u in range(a, b, HALF):
+                ysb[e, u] = (results, u - a)
+            sums, first = yacc[e, a]
+            nc.scalar.copy(results[:], sums[:, first : first + b - a])
 
         def scatter(e, a=0, b=C):
+            results, first = ysb[e, a]
             window = out_sb[:].indirect(lists[0][:, (e * C + a) // LIST_ROWS : (e * C + b) // LIST_ROWS])
-            nc.vector.tensor_tensor(window, ysb[e][:, a:b], gate_sb[:, e * C + a : e * C + b], MULT)
+            nc.vector.tensor_tensor(window, results[:, first : first + b - a], gate_sb[:, e * C + a : e * C + b], MULT)
 
         on_scalar, on_vector = nc.scalar.copy, nc.vector.tensor_copy
-
-        def round_shared(m):
-            round_first(m, 0, on_scalar)
-            round_first(m, 1, on_vector)
 
         gather(xs, U8, scales, "gs")
         gather(xw, U32, words, "gw")
@@ -174,50 +179,46 @@ def tile_moe_duo_relu_kernel(tc, x_words, x_scales, w1, wp, w2, gate, offs, offs
             round_first(m, 0, on_scalar)
             round_first(m, 1, on_scalar)
             quantize_first(m)
+            first_layer(m)
             if m == 1:
-                first_layer(0)
                 round_second(0, on_scalar)
                 quantize_second(0)
 
-        round_shared(3)
+        def shared(m, parts=2):
+            round_first(m, 0, on_scalar)
+            round_first(m, 1, on_vector, parts=2)
+            quantize_first(m, parts=parts)
+            first_layer(m)
+
+        shared(3)
         round_second(1, on_scalar)
-        quantize_first(3)
-        first_layer(1)
         quantize_second(1)
 
-        round_shared(4)
+        shared(4)
         relu(0, piece_area(4, 0))
-        quantize_first(4)
         second_layer(0)
 
-        round_shared(FIRST_SCATTER_AT)
-        copy_out(0, piece_area(FIRST_SCATTER_AT, 0) + HIDDEN_BYTES)
-        relu(1, piece_area(FIRST_SCATTER_AT, 0))
+        shared(5)
+        copy_out(0, at=piece_area(5, 0) + HIDDEN_BYTES)
+        relu(1, piece_area(5, 0))
         scatter(0)
-        quantize_first(FIRST_SCATTER_AT)
-        first_layer(2)
 
-        round_shared(6)
+        shared(6)
         second_layer(1)
-        quantize_first(6)
 
-        round_shared(7)
+        shared(7, parts=PACK)
         relu(2, piece_area(7, 0))
-        copy_out(1, piece_area(7, 0) + HIDDEN_BYTES)
+        copy_out(1, at=piece_area(7, 0) + HIDDEN_BYTES)
         round_second(2, on_vector)
-        quantize_first(7, parts=PACK)
-        first_layer(3)
         quantize_second(2)
         second_layer(2)
         round_second(3, on_scalar)
-
         scatter(1)
         quantize_second(3)
         relu(3)
-        copy_out(2)
         second_layer(3)
-        scatter(2, 0, HALF)
-        scatter(2, HALF, C)
+        copy_out(2)
+        scatter(2)
         copy_out(3)
         scatter(3)
         nc.sync.dma_start(out, out_sb[:])

@@ -121,23 +121,34 @@ def tile_moe_duo_relu_kernel(tc, x_words, x_scales, w1, wp, w2, gate, offs, offs
                 b = a + PACK // parts
                 quantize(wc[m][:, a * P : b * P], ws[m][:, a * P : b * P], rounded[m][:, a:b].rearrange("p t q j -> p (t q j)"))
 
-        def first_layer(m):
-            e, side = divmod(m, 2)
-            if side == 0:
-                for u in range(2):
-                    acc[e, u] = hpsum.tile([P, PACK, HALF], F32, name="acc")
+        def product(e, u, t, side, start, stop):
+            m = 2 * e + side
+            slots = slice((e % 2) * C + u * HALF, (e % 2) * C + (u + 1) * HALF)
+            nc.tensor.matmul_mx(
+                out=acc[e, u][:, t, :],
+                lhsT=wc[m][:, t * P : (t + 1) * P].bitcast(FP8X4),
+                lhsT_scale=ws[m][:, t * P : (t + 1) * P],
+                rhs=words[e // 2, side][:, slots].bitcast(FP8X4),
+                rhs_scale=scales[e // 2, side][:, slots],
+                start=start,
+                stop=stop,
+            )
+
+        def banks(e):
+            for u in range(2):
+                acc[e, u] = hpsum.tile([P, PACK, HALF], F32, name="acc")
+
+        def first_layer(e):
+            banks(e)
+            for u in range(2):
+                for t in range(PACK):
+                    for side in range(2):
+                        product(e, u, t, side, side == 0, side == 1)
+
+        def first_layer_side(e, side):
             for t in range(PACK):
                 for u in range(2):
-                    slots = slice((e % 2) * C + u * HALF, (e % 2) * C + (u + 1) * HALF)
-                    nc.tensor.matmul_mx(
-                        out=acc[e, u][:, t, :],
-                        lhsT=wc[m][:, t * P : (t + 1) * P].bitcast(FP8X4),
-                        lhsT_scale=ws[m][:, t * P : (t + 1) * P],
-                        rhs=words[e // 2, side][:, slots].bitcast(FP8X4),
-                        rhs_scale=scales[e // 2, side][:, slots],
-                        start=(side == 0 and t == 0),
-                        stop=(side == 1 and t == PACK - 1),
-                    )
+                    product(e, u, t, side, side == 0 and t == 0, side == 1 and t == PACK - 1)
 
         def relu(e, at=None, a=0, b=C):
             hb[e, a] = placed([P, b - a, PACK], BF16, "hb%d_%d" % (e, a), at)
@@ -179,34 +190,42 @@ def tile_moe_duo_relu_kernel(tc, x_words, x_scales, w1, wp, w2, gate, offs, offs
             round_first(m, 0, on_scalar)
             round_first(m, 1, on_scalar)
             quantize_first(m)
-            first_layer(m)
             if m == 1:
+                first_layer(0)
                 round_second(0, on_scalar)
                 quantize_second(0)
 
-        def shared(m, parts=2):
+        def round_shared(m, parts=2):
             round_first(m, 0, on_scalar)
-            round_first(m, 1, on_vector, parts=2)
-            quantize_first(m, parts=parts)
-            first_layer(m)
+            round_first(m, 1, on_vector, parts=parts)
 
-        shared(3)
+        round_shared(3)
+        quantize_first(3, parts=2)
+        first_layer(1)
         round_second(1, on_scalar)
+        relu(0, second_area(1))
         quantize_second(1)
-
-        shared(4)
-        relu(0, piece_area(4, 0))
         second_layer(0)
 
-        shared(5)
-        copy_out(0, at=piece_area(5, 0) + HIDDEN_BYTES)
+        round_shared(4)
+        copy_out(0, at=piece_area(4, 0))
+        quantize_first(4, parts=2)
+
+        round_shared(5, parts=1)
         relu(1, piece_area(5, 0))
         scatter(0)
+        quantize_first(5)
+        first_layer(2)
 
-        shared(6)
+        round_shared(6)
+        quantize_first(6, parts=2)
         second_layer(1)
+        banks(3)
+        first_layer_side(3, 0)
 
-        shared(7, parts=PACK)
+        round_shared(7)
+        quantize_first(7, parts=PACK)
+        first_layer_side(3, 1)
         relu(2, piece_area(7, 0))
         copy_out(1, at=piece_area(7, 0) + HIDDEN_BYTES)
         round_second(2, on_vector)

@@ -23,6 +23,7 @@ COLS = H // 2
 MATRICES = 2 * E
 AREA = PACK * COLS * 4
 FIRST_SCATTER_AT = 5
+LAST_W1, LAST_WP = MATRICES - 2, MATRICES - 1
 HIDDEN_BYTES = C * PACK * 2
 
 
@@ -46,6 +47,8 @@ def tile_moe_duo_relu_kernel(tc, x_words, x_scales, w1, wp, w2, gate, offs, offs
         def second_area(e):
             return (2 * MATRICES + e) * AREA
 
+        last_w1_area = second_area(E)
+
         def placed(shape, dtype, name, at=None):
             if at is None:
                 return keep.tile(shape, dtype, name=name, align_bytes=64)
@@ -63,7 +66,7 @@ def tile_moe_duo_relu_kernel(tc, x_words, x_scales, w1, wp, w2, gate, offs, offs
             nc.sync.dma_start(raw2[e][:], w2[e].rearrange("(p j) n -> p j n", j=PACK))
 
         def load_gate(first, end):
-            nc.sync.dma_start(gate_sb[:, first * HALF : end * HALF], gate[:, first * HALF : end * HALF])
+            nc.sync.dma_start(gate_sb[:, first * C : end * C], gate[:, first * C : end * C])
 
         nc.sync.dma_start(lists[0][:], offs)
         for q in range(4):
@@ -76,12 +79,12 @@ def tile_moe_duo_relu_kernel(tc, x_words, x_scales, w1, wp, w2, gate, offs, offs
                 nc.sync.dma_start(xw[:].bitcast(I32), x_words[0].rearrange("p t d -> p (t d)").bitcast(I32))
             load_first(m, 1)
             if m == FIRST_SCATTER_AT:
-                load_gate(0, 2)
+                load_gate(0, 1)
             if m in (1, 3):
                 load_second(m // 2)
         load_second(2)
         load_second(3)
-        load_gate(2, 8)
+        load_gate(1, E)
 
         words, scales = {}, {}
 
@@ -95,7 +98,8 @@ def tile_moe_duo_relu_kernel(tc, x_words, x_scales, w1, wp, w2, gate, offs, offs
         def tiles(count, shape, dtype, label):
             return [placed(shape, dtype, "%s%d" % (label, i)) for i in range(count)]
 
-        rounded, wc, ws = tiles(MATRICES, [P, PACK, P, PACK], BF16, "grp"), tiles(MATRICES, [P, H], U32, "wc"), tiles(MATRICES, [P, H], U8, "ws")
+        rounded = [placed([P, PACK, P, PACK], BF16, "grp%d" % m, last_w1_area if m == LAST_W1 else None) for m in range(MATRICES)]
+        wc, ws = tiles(MATRICES, [P, H], U32, "wc"), tiles(MATRICES, [P, H], U8, "ws")
         rounded2, w2c, w2s = tiles(E, [P, N, PACK], BF16, "grp2_"), tiles(E, [P, N], U32, "w2c"), tiles(E, [P, N], U8, "w2s")
         hc, hs = tiles(E, [P, C], U32, "hc"), tiles(E, [P, C], U8, "hs")
         hb, ysb, acc, yacc = {}, {}, {}, {}
@@ -150,39 +154,37 @@ def tile_moe_duo_relu_kernel(tc, x_words, x_scales, w1, wp, w2, gate, offs, offs
                 for u in range(2):
                     product(e, u, t, side, side == 0 and t == 0, side == 1 and t == PACK - 1)
 
-        def relu(e, at=None, a=0, b=C):
-            hb[e, a] = placed([P, b - a, PACK], BF16, "hb%d_%d" % (e, a), at)
-            for u in range(a, b, HALF):
-                nc.scalar.activation(hb[e, a][:, u - a : u - a + HALF, :], acc[e, u // HALF][:].rearrange("p t n -> p n t"), RELU)
+        def relu(e, at=None):
+            hb[e] = placed([P, C, PACK], BF16, "hb%d" % e, at)
+            for u in range(2):
+                nc.scalar.activation(hb[e][:, u * HALF : (u + 1) * HALF, :], acc[e, u][:].rearrange("p t n -> p n t"), RELU)
 
-        def second_layer(e, a=0, b=C):
-            quantize(hc[e][:, a:b], hs[e][:, a:b], hb[e, a][:].rearrange("p n t -> p (n t)"))
-            sums = ypsum.tile([P, b - a], F32, name="yacc")
-            for u in range(a, b, HALF):
-                yacc[e, u] = (sums, u - a)
+        def second_layer(e):
+            quantize(hc[e][:], hs[e][:], hb[e][:].rearrange("p n t -> p (n t)"))
+            yacc[e] = ypsum.tile([P, C], F32, name="yacc")
             nc.tensor.matmul_mx(
-                out=sums[:],
+                out=yacc[e][:],
                 lhsT=w2c[e][:].bitcast(FP8X4),
                 lhsT_scale=w2s[e][:],
-                rhs=hc[e][:, a:b].bitcast(FP8X4),
-                rhs_scale=hs[e][:, a:b],
+                rhs=hc[e][:].bitcast(FP8X4),
+                rhs_scale=hs[e][:],
                 start=True,
                 stop=True,
             )
 
-        def copy_out(e, a=0, b=C, at=None):
-            results = placed([P, b - a], F32, "ysb%d_%d" % (e, a), at)
-            for u in range(a, b, HALF):
-                ysb[e, u] = (results, u - a)
-            sums, first = yacc[e, a]
-            nc.scalar.copy(results[:], sums[:, first : first + b - a])
+        def copy_out(e, at=None):
+            ysb[e] = placed([P, C], F32, "ysb%d" % e, at)
+            nc.scalar.copy(ysb[e][:], yacc[e][:])
 
-        def scatter(e, a=0, b=C):
-            results, first = ysb[e, a]
-            window = out_sb[:].indirect(lists[0][:, (e * C + a) // LIST_ROWS : (e * C + b) // LIST_ROWS])
-            nc.vector.tensor_tensor(window, results[:, first : first + b - a], gate_sb[:, e * C + a : e * C + b], MULT)
+        def scatter(e):
+            window = out_sb[:].indirect(lists[0][:, e * C // LIST_ROWS : (e + 1) * C // LIST_ROWS])
+            nc.vector.tensor_tensor(window, ysb[e][:], gate_sb[:, e * C : (e + 1) * C], MULT)
 
         on_scalar, on_vector = nc.scalar.copy, nc.vector.tensor_copy
+
+        def round_shared(m, parts=1):
+            round_first(m, 0, on_scalar)
+            round_first(m, 1, on_vector, parts)
 
         gather(xs, U8, scales, "gs")
         gather(xw, U32, words, "gw")
@@ -195,11 +197,7 @@ def tile_moe_duo_relu_kernel(tc, x_words, x_scales, w1, wp, w2, gate, offs, offs
                 round_second(0, on_scalar)
                 quantize_second(0)
 
-        def round_shared(m, parts=2):
-            round_first(m, 0, on_scalar)
-            round_first(m, 1, on_vector, parts=parts)
-
-        round_shared(3)
+        round_shared(3, parts=2)
         quantize_first(3, parts=2)
         first_layer(1)
         round_second(1, on_scalar)
@@ -207,31 +205,32 @@ def tile_moe_duo_relu_kernel(tc, x_words, x_scales, w1, wp, w2, gate, offs, offs
         quantize_second(1)
         second_layer(0)
 
-        round_shared(4)
-        copy_out(0, at=piece_area(4, 0))
+        round_shared(4, parts=2)
+        copy_out(0)
         quantize_first(4, parts=2)
 
-        round_shared(5, parts=1)
-        relu(1, piece_area(5, 0))
+        round_shared(FIRST_SCATTER_AT)
+        relu(1, piece_area(FIRST_SCATTER_AT, 0))
         scatter(0)
-        quantize_first(5)
+        quantize_first(FIRST_SCATTER_AT)
         first_layer(2)
 
-        round_shared(6)
-        quantize_first(6, parts=2)
+        round_shared(LAST_W1)
+        quantize_first(LAST_W1)
         second_layer(1)
-        banks(3)
-        first_layer_side(3, 0)
+        banks(E - 1)
+        first_layer_side(E - 1, 0)
 
-        round_shared(7)
-        quantize_first(7, parts=PACK)
-        first_layer_side(3, 1)
-        relu(2, piece_area(7, 0))
-        copy_out(1, at=piece_area(7, 0) + HIDDEN_BYTES)
+        round_shared(LAST_WP, parts=2)
+        quantize_first(LAST_WP, parts=2)
+        first_layer_side(E - 1, 1)
+        relu(2, last_w1_area)
+        copy_out(1, last_w1_area + HIDDEN_BYTES)
         round_second(2, on_vector)
         quantize_second(2)
         second_layer(2)
         round_second(3, on_scalar)
+
         scatter(1)
         quantize_second(3)
         relu(3)

@@ -68,11 +68,12 @@ def tile_moe_duo_relu_kernel(tc, x_words, x_scales, w1, wp, w2, gate, offs, offs
         def load_gate(first, end):
             nc.sync.dma_start(gate_sb[:, first * C : end * C], gate[:, first * C : end * C])
 
+        nc.gpsimd.memset(xs[:].bitcast(I32), 0)
         nc.sync.dma_start(lists[0][:], offs)
+        nc.sync.dma_start(lists[1][:], offs2)
         for q in range(4):
             rows = x_scales[0, 4 * q : 4 * q + 4, :].bitcast(I32)
-            nc.sync.dma_start(xs[32 * q : 32 * q + 32, :].bitcast(I32), rows.partition_broadcast(8))
-        nc.sync.dma_start(lists[1][:], offs2)
+            nc.sync.dma_start(xs[32 * q : 32 * q + 4, :].bitcast(I32), rows)
         for m in range(MATRICES):
             load_first(m, 0)
             if m == 0:
@@ -84,7 +85,8 @@ def tile_moe_duo_relu_kernel(tc, x_words, x_scales, w1, wp, w2, gate, offs, offs
                 load_second(m // 2)
         load_second(2)
         load_second(3)
-        load_gate(1, E)
+        load_gate(1, 2)
+        load_gate(2, E)
 
         words, scales = {}, {}
 

from contextlib import ExitStack

import concourse.mybir as mybir

K, T, E, C, H, N = 512, 1024, 4, 256, 512, 128
FLOPS = 2 * E * C * (2 * K * H + H * N)

F32 = mybir.dt.float32
BF16 = mybir.dt.bfloat16
I32 = mybir.dt.int32
U32 = mybir.dt.uint32
U16 = mybir.dt.uint16
U8 = mybir.dt.uint8
FP8X4 = mybir.dt.float8_e4m3fn_x4
RELU = mybir.ActivationFunctionType.Relu
MULT = mybir.AluOpType.mult

P = 128
PACK = 4
LIST_ROWS = 16
HALF = C // 2
COLS = H // 2
MATRICES = 2 * E
AREA = PACK * COLS * 4
FIRST_SCATTER_AT = 5
LAST_W1, LAST_WP = MATRICES - 2, MATRICES - 1
HIDDEN_BYTES = C * PACK * 2


def tile_moe_duo_relu_kernel(tc, x_words, x_scales, w1, wp, w2, gate, offs, offs2, out):
    nc = tc.nc
    with ExitStack() as ctx:
        keep = ctx.enter_context(tc.tile_pool(name="keep", bufs=1))
        stage = ctx.enter_context(tc.tile_pool(name="stage", bufs=1))
        hpsum = ctx.enter_context(tc.psum_pool(name="hpsum", bufs=6))
        ypsum = ctx.enter_context(tc.psum_pool(name="ypsum", bufs=2))

        lists = [keep.tile([P, T // LIST_ROWS], U16, name="offs_sb"), keep.tile([P, T // LIST_ROWS], U16, name="offs2_sb")]
        xw = keep.tile([P, T], U32, name="xw", align_bytes=64)
        xs = keep.tile([P, T], U8, name="xs", align_bytes=64)
        gate_sb = keep.tile([P, E * C], F32, name="gate_sb", align_bytes=64)
        out_sb = keep.tile([P, T], F32, name="out_sb", align_bytes=64)

        def piece_area(m, piece):
            return (2 * m + piece) * AREA

        def second_area(e):
            return (2 * MATRICES + e) * AREA

        last_w1_area = second_area(E)

        def placed(shape, dtype, name, at=None):
            if at is None:
                return keep.tile(shape, dtype, name=name, align_bytes=64)
            return stage.tile(shape, dtype, name=name, align_bytes=64, offset=at)

        raw, raw2 = {}, {}

        def load_first(m, piece):
            rows = (w1, wp)[m % 2][m // 2].rearrange("(p j) c -> p j c", j=PACK)
            raw[m, piece] = placed([P, PACK, COLS], F32, "raw%d%d" % (m, piece), piece_area(m, piece))
            nc.sync.dma_start(raw[m, piece][:], rows[:, :, piece * COLS : (piece + 1) * COLS])

        def load_second(e):
            raw2[e] = placed([P, PACK, N], F32, "raw2_%d" % e, second_area(e))
            nc.sync.dma_start(raw2[e][:], w2[e].rearrange("(p j) n -> p j n", j=PACK))

        def load_gate(first, end):
            nc.sync.dma_start(gate_sb[:, first * C : end * C], gate[:, first * C : end * C])

        nc.gpsimd.memset(xs[:].bitcast(I32), 0)
        nc.sync.dma_start(lists[0][:], offs)
        nc.sync.dma_start(lists[1][:], offs2)
        for q in range(4):
            rows = x_scales[0, 4 * q : 4 * q + 4, :].bitcast(I32)
            nc.sync.dma_start(xs[32 * q : 32 * q + 4, :].bitcast(I32), rows)
        for m in range(MATRICES):
            load_first(m, 0)
            if m == 0:
                nc.sync.dma_start(xw[:].bitcast(I32), x_words[0].rearrange("p t d -> p (t d)").bitcast(I32))
            load_first(m, 1)
            if m == FIRST_SCATTER_AT:
                load_gate(0, 1)
            if m in (1, 3):
                load_second(m // 2)
        load_second(2)
        load_second(3)
        load_gate(1, 2)
        load_gate(2, E)

        words, scales = {}, {}

        def gather(table, dtype, into, label):
            for pair in range(E // 2):
                cols = slice(pair * 2 * C // LIST_ROWS, (pair + 1) * 2 * C // LIST_ROWS)
                for side in range(2):
                    into[pair, side] = placed([P, 2 * C], dtype, "%s%d%d" % (label, pair, side))
                    nc.vector.tensor_copy(into[pair, side][:], table[:].indirect(lists[side][:, cols]))

        def tiles(count, shape, dtype, label):
            return [placed(shape, dtype, "%s%d" % (label, i)) for i in range(count)]

        rounded = [placed([P, PACK, P, PACK], BF16, "grp%d" % m, last_w1_area if m == LAST_W1 else None) for m in range(MATRICES)]
        wc, ws = tiles(MATRICES, [P, H], U32, "wc"), tiles(MATRICES, [P, H], U8, "ws")
        rounded2, w2c, w2s = tiles(E, [P, N, PACK], BF16, "grp2_"), tiles(E, [P, N], U32, "w2c"), tiles(E, [P, N], U8, "w2s")
        hc, hs = tiles(E, [P, C], U32, "hc"), tiles(E, [P, C], U8, "hs")
        hb, ysb, acc, yacc = {}, {}, {}, {}

        def round_first(m, piece, copy, parts=1):
            src = raw[m, piece][:].rearrange("p j (q t) -> p q j t", t=PACK)
            groups = slice(piece * COLS // PACK, (piece + 1) * COLS // PACK)
            for a in range(0, PACK, PACK // parts):
                b = a + PACK // parts
                copy(rounded[m][:, a:b, groups, :].rearrange("p t q j -> p q j t"), src[:, :, :, a:b])

        def round_second(e, copy):
            copy(rounded2[e][:].rearrange("p (c i) j -> p c j i", i=4), raw2[e][:].rearrange("p j (c i) -> p c j i", i=4))

        def quantize(codes, plane, values):
            nc.vector.quantize_mx(out=codes.bitcast(FP8X4), scales=plane, in_=values)

        def quantize_second(e):
            quantize(w2c[e][:], w2s[e][:], rounded2[e][:].rearrange("p n j -> p (n j)"))

        def quantize_first(m, parts=1):
            for a in range(0, PACK, PACK // parts):
                b = a + PACK // parts
                quantize(wc[m][:, a * P : b * P], ws[m][:, a * P : b * P], rounded[m][:, a:b].rearrange("p t q j -> p (t q j)"))

        def product(e, u, t, side, start, stop):
            m = 2 * e + side
            slots = slice((e % 2) * C + u * HALF, (e % 2) * C + (u + 1) * HALF)
            nc.tensor.matmul_mx(
                out=acc[e, u][:, t, :],
                lhsT=wc[m][:, t * P : (t + 1) * P].bitcast(FP8X4),
                lhsT_scale=ws[m][:, t * P : (t + 1) * P],
                rhs=words[e // 2, side][:, slots].bitcast(FP8X4),
                rhs_scale=scales[e // 2, side][:, slots],
                start=start,
                stop=stop,
            )

        def banks(e):
            for u in range(2):
                acc[e, u] = hpsum.tile([P, PACK, HALF], F32, name="acc")

        def first_layer(e):
            banks(e)
            for u in range(2):
                for t in range(PACK):
                    for side in range(2):
                        product(e, u, t, side, side == 0, side == 1)

        def first_layer_side(e, side):
            for t in range(PACK):
                for u in range(2):
                    product(e, u, t, side, side == 0 and t == 0, side == 1 and t == PACK - 1)

        def relu(e, at=None):
            hb[e] = placed([P, C, PACK], BF16, "hb%d" % e, at)
            for u in range(2):
                nc.scalar.activation(hb[e][:, u * HALF : (u + 1) * HALF, :], acc[e, u][:].rearrange("p t n -> p n t"), RELU)

        def second_layer(e):
            quantize(hc[e][:], hs[e][:], hb[e][:].rearrange("p n t -> p (n t)"))
            yacc[e] = ypsum.tile([P, C], F32, name="yacc")
            nc.tensor.matmul_mx(
                out=yacc[e][:],
                lhsT=w2c[e][:].bitcast(FP8X4),
                lhsT_scale=w2s[e][:],
                rhs=hc[e][:].bitcast(FP8X4),
                rhs_scale=hs[e][:],
                start=True,
                stop=True,
            )

        def copy_out(e, at=None):
            ysb[e] = placed([P, C], F32, "ysb%d" % e, at)
            nc.scalar.copy(ysb[e][:], yacc[e][:])

        def scatter(e):
            window = out_sb[:].indirect(lists[0][:, e * C // LIST_ROWS : (e + 1) * C // LIST_ROWS])
            nc.vector.tensor_tensor(window, ysb[e][:], gate_sb[:, e * C : (e + 1) * C], MULT)

        on_scalar, on_vector = nc.scalar.copy, nc.vector.tensor_copy

        def round_shared(m, parts=1):
            round_first(m, 0, on_scalar)
            round_first(m, 1, on_vector, parts)

        gather(xs, U8, scales, "gs")
        gather(xw, U32, words, "gw")
        for m in range(3):
            round_first(m, 0, on_scalar)
            round_first(m, 1, on_scalar)
            quantize_first(m)
            if m == 1:
                first_layer(0)
                round_second(0, on_scalar)
                quantize_second(0)

        round_shared(3, parts=2)
        quantize_first(3, parts=2)
        first_layer(1)
        round_second(1, on_scalar)
        relu(0, second_area(1))
        quantize_second(1)
        second_layer(0)

        round_shared(4, parts=2)
        copy_out(0)
        quantize_first(4, parts=2)

        round_shared(FIRST_SCATTER_AT)
        relu(1, piece_area(FIRST_SCATTER_AT, 0))
        scatter(0)
        quantize_first(FIRST_SCATTER_AT)
        first_layer(2)

        round_shared(LAST_W1)
        quantize_first(LAST_W1)
        second_layer(1)
        banks(E - 1)
        first_layer_side(E - 1, 0)

        round_shared(LAST_WP, parts=2)
        quantize_first(LAST_WP, parts=2)
        first_layer_side(E - 1, 1)
        relu(2, last_w1_area)
        copy_out(1, last_w1_area + HIDDEN_BYTES)
        round_second(2, on_vector)
        quantize_second(2)
        second_layer(2)
        round_second(3, on_scalar)

        scatter(1)
        quantize_second(3)
        relu(3)
        second_layer(3)
        copy_out(2)
        scatter(2)
        copy_out(3)
        scatter(3)
        nc.sync.dma_start(out, out_sb[:])
